import numpy as np
import ml_dtypes


def mxq(x, axis, fmt="e4m3"):
    dtype, down = {"e4m3": (ml_dtypes.float8_e4m3fn, 7), "e5m2": (ml_dtypes.float8_e5m2, 14)}[fmt]
    v = np.moveaxis(np.asarray(x, np.float32).astype(ml_dtypes.bfloat16).astype(np.float64), axis, -1)
    blocks = v.reshape(v.shape[:-1] + (-1, 32))
    amax = np.abs(blocks).max(-1, keepdims=True)
    byte = np.maximum(np.where(amax > 0, np.frexp(amax)[1] - 1 + 127, 0) - down, 1)
    scale = np.exp2(byte - 127.0)
    codes = (blocks / scale).astype(np.float32).astype(dtype).astype(np.float64)
    return np.moveaxis((codes * scale).reshape(v.shape), -1, axis)


WIDE = False


def mx_kscale(k):
    if not WIDE:
        return np.ones(k)
    levels = np.array([10, -10, 5, -5, 0])
    if k % 512:
        return np.exp2(np.random.permutation(np.resize(levels, k // 32))).repeat(32)
    a = np.empty((k // 512, 16))
    for p in range(k // 512):
        a[p, :8] = np.random.permutation(np.resize(levels, 8))
        for g in range(8):
            far = levels[np.abs(levels - a[p, g]) >= 10]
            a[p, g + 8] = far[np.random.randint(len(far))]
    return np.exp2(a.ravel()).repeat(32)


def f64(x):
    return np.asarray(x).astype(np.float64)


def striped(idx):
    return np.tile(idx.reshape(-1, 16).T, (8, 1)).astype(np.uint16)


def unstriped(offs):
    return offs[:16].T.reshape(-1).astype(np.int64)


def pack_weight(w):
    k, n = w.shape
    w = f64(np.asarray(w, np.float32).astype(ml_dtypes.bfloat16)).reshape(k // 32, 32, n)
    amax = np.abs(w).max(1)
    byte = np.clip(np.where(amax > 0, np.frexp(amax)[1] - 1 + 127 - 7, 1), 1, 254)
    scaled = (w * np.exp2(127.0 - byte)[:, None, :]).reshape(k, n).astype(np.float32)
    words = np.ascontiguousarray(scaled.reshape(k // 512, 128, 4, n).transpose(0, 1, 3, 2)).astype(ml_dtypes.float8_e4m3fn).view(np.uint8)
    return words, np.ascontiguousarray(byte.astype(np.uint8).reshape(k // 512, 16, n))


def unpack_weight(words, scales):
    g, p, n, _ = words.shape
    vals = np.ascontiguousarray(words).view(ml_dtypes.float8_e4m3fn).astype(np.float64) * np.repeat(np.exp2(scales.astype(np.float64) - 127.0), 8, axis=1)[..., None]
    return vals.transpose(0, 1, 3, 2).reshape(g * 512, n)


K, T, S, N, V = 512, 2048, 512, 128, 256
P = 2 ** 7


def setup_inputs():
    n = np.random.standard_normal
    s = mx_kscale(K)[:, None]
    packed_xT = pack_weight(n((K, T)) * s)
    return {
        "x_words": packed_xT[0],
        "x_scales": packed_xT[1],
        "w1": (n((K, N)) / np.sqrt(K) / s).astype(np.float32),
        "w2": (n((K, N)) / np.sqrt(K) / s).astype(np.float32),
        "w3": (n((K, N)) / np.sqrt(K) / s).astype(np.float32),
        "sn": (np.tile(np.where(np.random.uniform(size=S) < 0.5, 1.0, -1.0), (P, 1))).astype(np.float32),
        "sa": (np.tile(np.where(np.random.uniform(size=V) < 0.5, 1.0, -1.0), (P, 1))).astype(np.float32),
        "sb": (np.tile(np.where(np.random.uniform(size=V) < 0.5, 1.0, -1.0), (P, 1))).astype(np.float32),
        "sf": (np.tile(np.where(np.random.uniform(size=S) < 0.5, 1.0, -1.0), (P, 1))).astype(np.float32),
        "offs": striped(np.random.permutation(T)[:S]),
        "inc": striped(np.random.permutation(S)),
        "head": striped(np.random.permutation(np.concatenate([np.arange(V), np.random.randint(0, V, S - V)]))),
        "tail": striped(np.random.permutation(np.concatenate([np.arange(V), np.random.randint(0, V, S - V)]))),
        "tri": striped(np.random.permutation(S)[:V]),
        "trj": striped(np.random.permutation(S)[:V]),
        "face": striped(np.random.permutation(np.concatenate([np.arange(V), np.random.randint(0, V, S - V)]))),
    }


def reference(x_words, x_scales, w1, w2, w3, sn, sa, sb, sf, offs, inc, head, tail, tri, trj, face):
    xq = unpack_weight(x_words, x_scales)[:, unstriped(offs)]
    own = mxq(f64(w3), 0, "e4m3").T @ xq
    y = mxq(f64(w1), 0, "e4m3").T @ xq
    li = y[:, unstriped(inc)] * f64(sn)[:1]
    dv = li.reshape(len(li), -1, 2).sum(axis=2)
    down = dv[:, unstriped(head)] - dv[:, unstriped(tail)]
    h = mxq(f64(w2), 0, "e4m3").T @ xq
    cu = h[:, unstriped(tri)] * f64(sa)[:1] + h[:, unstriped(trj)] * f64(sb)[:1]
    up = cu[:, unstriped(face)] * f64(sf)[:1]
    return own + down + up

@@ -1,0 +1,140 @@
+from contextlib import ExitStack
+
+import concourse.mybir as mybir
+
+K, T, S, N, V = 512, 2048, 512, 128, 256
+FLOPS = 3 * 2 * K * N * S
+
+F32 = mybir.dt.float32
+BF16 = mybir.dt.bfloat16
+I32 = mybir.dt.int32
+U32 = mybir.dt.uint32
+U16 = mybir.dt.uint16
+U8 = mybir.dt.uint8
+FP8X4 = mybir.dt.float8_e4m3fn_x4
+MULT = mybir.AluOpType.mult
+ADD = mybir.AluOpType.add
+SUB = mybir.AluOpType.subtract
+
+P = 128
+PACK = 4
+HALF = S // 2
+LCOL = 16
+
+
+def tile_picked_yhodge_none_p_kernel(tc, x_words, x_scales, w1, w2, w3, sn, sa, sb, sf, offs, inc, head, tail, tri, trj, face, out):
+    nc = tc.nc
+    with ExitStack() as ctx:
+        lists = ctx.enter_context(tc.tile_pool(name="lists", bufs=1))
+        sb_pool = ctx.enter_context(tc.tile_pool(name="work", bufs=1))
+        psum = ctx.enter_context(tc.psum_pool(name="psum", bufs=1))
+
+        def load_list(name, src):
+            t = lists.tile(list(src.shape), U16, name=name)
+            nc.sync.dma_start(t[:], src)
+            return t
+
+        def load_f32(name, src):
+            t = sb_pool.tile(list(src.shape), F32, name=name)
+            nc.sync.dma_start(t[:], src)
+            return t
+
+        def load_w(name, src):
+            t = sb_pool.tile([P, PACK, N], F32, name=name)
+            nc.sync.dma_start(t[:], src.rearrange("(p j) n -> p j n", j=PACK))
+            return t
+
+        def half_list(t, i):
+            return t[:, i * HALF // LCOL : (i + 1) * HALF // LCOL]
+
+        def half(t, i):
+            return t[:, i * HALF : (i + 1) * HALF]
+
+        xs = sb_pool.tile([P, T], U8, name="xs", align_bytes=64)
+        nc.vector.memset(xs[:].bitcast(I32), 0)
+        dv = sb_pool.tile([P, 2 * V], F32, name="dv")
+        cu = sb_pool.tile([P, 2 * V], F32, name="cu")
+        nc.vector.memset(dv[:, V:], 0.0)
+        nc.vector.memset(cu[:, V:], 0.0)
+        for q in range(4):
+            nc.scalar.dma_start(xs[32 * q : 32 * q + 4, :].bitcast(I32), x_scales[0, 4 * q : 4 * q + 4, :].bitcast(I32))
+
+        w2_raw = load_w("w2_raw", w2)
+        offs_t = load_list("offs_t", offs)
+        xw = sb_pool.tile([P, T], U32, name="xw", align_bytes=64)
+        nc.sync.dma_start(xw[:].bitcast(I32), x_words[0].rearrange("p n t -> p (n t)").bitcast(I32))
+        w1_raw = load_w("w1_raw", w1)
+        tri_t = load_list("tri_t", tri)
+        trj_t = load_list("trj_t", trj)
+        sa_t = load_f32("sa_t", sa)
+        sb_t = load_f32("sb_t", sb)
+        inc_t = load_list("inc_t", inc)
+        sn_t = load_f32("sn_t", sn)
+        w3_raw = load_w("w3_raw", w3)
+        face_t = load_list("face_t", face)
+        sf_t = load_f32("sf_t", sf)
+        tail_t = load_list("tail_t", tail)
+        head_t = load_list("head_t", head)
+
+        def cast(name, raw, copy):
+            g = sb_pool.tile([P, N, PACK], BF16, name=name, align_bytes=64)
+            copy(g[:], raw[:].rearrange("p j n -> p n j"))
+            return g
+
+        def quant(name, g):
+            codes = sb_pool.tile([P, N], U32, name=name + "_c", align_bytes=64)
+            scales = sb_pool.tile([P, N], U8, name=name + "_s", align_bytes=64)
+            nc.vector.quantize_mx(out=codes[:].bitcast(FP8X4), scales=scales[:], in_=g[:].rearrange("p n j -> p (n j)"))
+            return codes, scales
+
+        def product(dst, w, words, scales):
+            nc.tensor.matmul_mx(out=dst, lhsT=w[0][:].bitcast(FP8X4), lhsT_scale=w[1][:],
+                                rhs=words.bitcast(FP8X4), rhs_scale=scales, start=True, stop=True)
+
+        w2_g = cast("w2_g", w2_raw, nc.vector.tensor_copy)
+        gs = sb_pool.tile([P, S], U8, name="gs", align_bytes=64)
+        nc.vector.tensor_copy(gs[:], xs[:].indirect(offs_t[:]))
+        w2_q = quant("w2_q", w2_g)
+
+        gw = sb_pool.tile([P, S], U32, name="gw", align_bytes=64)
+        h = sb_pool.tile([P, S], F32, name="h")
+        y = sb_pool.tile([P, S], F32, name="y")
+        for i in range(2):
+            nc.vector.tensor_copy(half(gw, i), xw[:].indirect(half_list(offs_t, i)))
+            h_ps = psum.tile([P, HALF], F32, name="h_ps%d" % i)
+            product(h_ps[:], w2_q, half(gw, i), half(gs, i))
+            nc.scalar.copy(half(h, i), h_ps[:])
+
+        w1_g = cast("w1_g", w1_raw, nc.vector.tensor_copy)
+        w1_q = quant("w1_q", w1_g)
+        y_ps = psum.tile([P, S], F32, name="y_ps")
+        product(y_ps[:], w1_q, gw[:], gs[:])
+        nc.scalar.copy(y[:], y_ps[:])
+
+        w3_g = cast("w3_g", w3_raw, nc.scalar.copy)
+
+        ta = sb_pool.tile([P, V], F32, name="ta")
+        tb = sb_pool.tile([P, V], F32, name="tb")
+        li = sb_pool.tile([P, S], F32, name="li")
+        up = sb_pool.tile([P, S], F32, name="up")
+        u = sb_pool.tile([P, S], F32, name="u")
+        c = sb_pool.tile([P, S], F32, name="c")
+        res = sb_pool.tile([P, S], F32, name="res")
+        nc.vector.tensor_tensor(ta[:], h[:].indirect(tri_t[:]), sa_t[:], MULT)
+        nc.vector.tensor_tensor(tb[:], h[:].indirect(trj_t[:]), sb_t[:], MULT)
+        nc.vector.tensor_tensor(half(li, 0), y[:].indirect(half_list(inc_t, 0)), half(sn_t, 0), MULT)
+        nc.vector.tensor_tensor(cu[:, :V], ta[:], tb[:], ADD)
+        w3_q = quant("w3_q", w3_g)
+        own_ps = psum.tile([P, S], F32, name="own_ps")
+        product(own_ps[:], w3_q, gw[:], gs[:])
+        nc.vector.tensor_tensor(half(li, 1), y[:].indirect(half_list(inc_t, 1)), half(sn_t, 1), MULT)
+        nc.vector.tensor_tensor(half(up, 0), cu[:].indirect(half_list(face_t, 0)), half(sf_t, 0), MULT)
+        nc.vector.tensor_tensor(dv[:, :V], li[:, 0::2], li[:, 1::2], ADD)
+        nc.vector.tensor_tensor(half(up, 1), cu[:].indirect(half_list(face_t, 1)), half(sf_t, 1), MULT)
+        for i in range(2):
+            nc.vector.tensor_tensor(half(u, i), half(up, i), half(own_ps, i), ADD)
+        for i in range(2):
+            nc.vector.tensor_tensor(half(c, i), dv[:].indirect(half_list(tail_t, i)), half(u, i), SUB)
+        for i in range(2):
+            nc.vector.tensor_tensor(half(res, i), dv[:].indirect(half_list(head_t, i)), half(c, i), SUB)
+            nc.sync.dma_start(out[:, i * HALF : (i + 1) * HALF], half(res, i))

@@ -56,21 +56,21 @@ def tile_picked_yhodge_none_p_kernel(tc, x_words, x_scales, w1, w2, w3, sn, sa, 
         cu = sb_pool.tile([P, 2 * V], F32, name="cu")
         nc.vector.memset(dv[:, V:], 0.0)
         nc.vector.memset(cu[:, V:], 0.0)
-        for q in range(4):
-            nc.scalar.dma_start(xs[32 * q : 32 * q + 4, :].bitcast(I32), x_scales[0, 4 * q : 4 * q + 4, :].bitcast(I32))
-
-        w2_raw = load_w("w2_raw", w2)
         offs_t = load_list("offs_t", offs)
+        w2_raw = load_w("w2_raw", w2)
+        for q in range(4):
+            queue = nc.sync if q < 2 else nc.scalar
+            queue.dma_start(xs[32 * q : 32 * q + 4, :].bitcast(I32), x_scales[0, 4 * q : 4 * q + 4, :].bitcast(I32))
         xw = sb_pool.tile([P, T], U32, name="xw", align_bytes=64)
         nc.sync.dma_start(xw[:].bitcast(I32), x_words[0].rearrange("p n t -> p (n t)").bitcast(I32))
-        w1_raw = load_w("w1_raw", w1)
         tri_t = load_list("tri_t", tri)
-        trj_t = load_list("trj_t", trj)
+        w1_raw = load_w("w1_raw", w1)
+        w3_raw = load_w("w3_raw", w3)
         sa_t = load_f32("sa_t", sa)
         sb_t = load_f32("sb_t", sb)
+        trj_t = load_list("trj_t", trj)
         inc_t = load_list("inc_t", inc)
         sn_t = load_f32("sn_t", sn)
-        w3_raw = load_w("w3_raw", w3)
         face_t = load_list("face_t", face)
         sf_t = load_f32("sf_t", sf)
         tail_t = load_list("tail_t", tail)
@@ -80,6 +80,9 @@ def tile_picked_yhodge_none_p_kernel(tc, x_words, x_scales, w1, w2, w3, sn, sa, 
             g = sb_pool.tile([P, N, PACK], BF16, name=name, align_bytes=64)
             copy(g[:], raw[:].rearrange("p j n -> p n j"))
             return g
+
+        def pool_copy(dst, src):
+            nc.gpsimd.tensor_scalar(dst, src, 1.0, 0.0, MULT, ADD)
 
         def quant(name, g):
             codes = sb_pool.tile([P, N], U32, name=name + "_c", align_bytes=64)
@@ -96,6 +99,7 @@ def tile_picked_yhodge_none_p_kernel(tc, x_words, x_scales, w1, w2, w3, sn, sa, 
         nc.vector.tensor_copy(gs[:], xs[:].indirect(offs_t[:]))
         w2_q = quant("w2_q", w2_g)
 
+        w3_g = cast("w3_g", w3_raw, pool_copy)
         gw = sb_pool.tile([P, S], U32, name="gw", align_bytes=64)
         h = sb_pool.tile([P, S], F32, name="h")
         y = sb_pool.tile([P, S], F32, name="y")
@@ -111,7 +115,9 @@ def tile_picked_yhodge_none_p_kernel(tc, x_words, x_scales, w1, w2, w3, sn, sa, 
         product(y_ps[:], w1_q, gw[:], gs[:])
         nc.scalar.copy(y[:], y_ps[:])
 
-        w3_g = cast("w3_g", w3_raw, nc.scalar.copy)
+        w3_q = quant("w3_q", w3_g)
+        own_ps = psum.tile([P, S], F32, name="own_ps")
+        product(own_ps[:], w3_q, gw[:], gs[:])
 
         ta = sb_pool.tile([P, V], F32, name="ta")
         tb = sb_pool.tile([P, V], F32, name="tb")
@@ -124,9 +130,6 @@ def tile_picked_yhodge_none_p_kernel(tc, x_words, x_scales, w1, w2, w3, sn, sa, 
         nc.vector.tensor_tensor(tb[:], h[:].indirect(trj_t[:]), sb_t[:], MULT)
         nc.vector.tensor_tensor(half(li, 0), y[:].indirect(half_list(inc_t, 0)), half(sn_t, 0), MULT)
         nc.vector.tensor_tensor(cu[:, :V], ta[:], tb[:], ADD)
-        w3_q = quant("w3_q", w3_g)
-        own_ps = psum.tile([P, S], F32, name="own_ps")
-        product(own_ps[:], w3_q, gw[:], gs[:])
         nc.vector.tensor_tensor(half(li, 1), y[:].indirect(half_list(inc_t, 1)), half(sn_t, 1), MULT)
         nc.vector.tensor_tensor(half(up, 0), cu[:].indirect(half_list(face_t, 0)), half(sf_t, 0), MULT)
         nc.vector.tensor_tensor(dv[:, :V], li[:, 0::2], li[:, 1::2], ADD)

@@ -52,10 +52,6 @@ def tile_picked_yhodge_none_p_kernel(tc, x_words, x_scales, w1, w2, w3, sn, sa, 
 
         xs = sb_pool.tile([P, T], U8, name="xs", align_bytes=64)
         nc.vector.memset(xs[:].bitcast(I32), 0)
-        dv = sb_pool.tile([P, 2 * V], F32, name="dv")
-        cu = sb_pool.tile([P, 2 * V], F32, name="cu")
-        nc.vector.memset(dv[:, V:], 0.0)
-        nc.vector.memset(cu[:, V:], 0.0)
         offs_t = load_list("offs_t", offs)
         w2_raw = load_w("w2_raw", w2)
         for q in range(4):
@@ -66,11 +62,12 @@ def tile_picked_yhodge_none_p_kernel(tc, x_words, x_scales, w1, w2, w3, sn, sa, 
         tri_t = load_list("tri_t", tri)
         w1_raw = load_w("w1_raw", w1)
         w3_raw = load_w("w3_raw", w3)
-        sa_t = load_f32("sa_t", sa)
-        sb_t = load_f32("sb_t", sb)
+        dv = sb_pool.tile([P, 2 * V], F32, name="dv")
+        nc.sync.dma_start(dv[:, :V], sa)
+        nc.sync.dma_start(dv[:, V:], sb)
         trj_t = load_list("trj_t", trj)
         inc_t = load_list("inc_t", inc)
-        sn_t = load_f32("sn_t", sn)
+        cu = load_f32("cu", sn)
         face_t = load_list("face_t", face)
         sf_t = load_f32("sf_t", sf)
         tail_t = load_list("tail_t", tail)
@@ -126,18 +123,19 @@ def tile_picked_yhodge_none_p_kernel(tc, x_words, x_scales, w1, w2, w3, sn, sa, 
         u = sb_pool.tile([P, S], F32, name="u")
         c = sb_pool.tile([P, S], F32, name="c")
         res = sb_pool.tile([P, S], F32, name="res")
-        nc.vector.tensor_tensor(ta[:], h[:].indirect(tri_t[:]), sa_t[:], MULT)
-        nc.vector.tensor_tensor(tb[:], h[:].indirect(trj_t[:]), sb_t[:], MULT)
-        nc.vector.tensor_tensor(half(li, 0), y[:].indirect(half_list(inc_t, 0)), half(sn_t, 0), MULT)
+        nc.vector.tensor_tensor(ta[:], h[:].indirect(tri_t[:]), dv[:, :V], MULT)
+        nc.vector.tensor_tensor(tb[:], h[:].indirect(trj_t[:]), dv[:, V:], MULT)
+        for i in (1, 0):
+            nc.vector.tensor_tensor(half(li, i), y[:].indirect(half_list(inc_t, i)), half(cu, i), MULT)
         nc.vector.tensor_tensor(cu[:, :V], ta[:], tb[:], ADD)
-        nc.vector.tensor_tensor(half(li, 1), y[:].indirect(half_list(inc_t, 1)), half(sn_t, 1), MULT)
-        nc.vector.tensor_tensor(half(up, 0), cu[:].indirect(half_list(face_t, 0)), half(sf_t, 0), MULT)
         nc.vector.tensor_tensor(dv[:, :V], li[:, 0::2], li[:, 1::2], ADD)
-        nc.vector.tensor_tensor(half(up, 1), cu[:].indirect(half_list(face_t, 1)), half(sf_t, 1), MULT)
+        for i in range(2):
+            nc.vector.tensor_tensor(half(up, i), cu[:].indirect(half_list(face_t, i)), half(sf_t, i), MULT)
         for i in range(2):
             nc.vector.tensor_tensor(half(u, i), half(up, i), half(own_ps, i), ADD)
         for i in range(2):
             nc.vector.tensor_tensor(half(c, i), dv[:].indirect(half_list(tail_t, i)), half(u, i), SUB)
         for i in range(2):
             nc.vector.tensor_tensor(half(res, i), dv[:].indirect(half_list(head_t, i)), half(c, i), SUB)
-            nc.sync.dma_start(out[:, i * HALF : (i + 1) * HALF], half(res, i))
+            queue = nc.sync if i == 0 else nc.scalar
+            queue.dma_start(out[:, i * HALF : (i + 1) * HALF], half(res, i))

@@ -66,10 +66,10 @@ def tile_picked_yhodge_none_p_kernel(tc, x_words, x_scales, w1, w2, w3, sn, sa, 
         nc.sync.dma_start(dv[:, :V], sa)
         nc.sync.dma_start(dv[:, V:], sb)
         trj_t = load_list("trj_t", trj)
-        inc_t = load_list("inc_t", inc)
         cu = load_f32("cu", sn)
-        face_t = load_list("face_t", face)
+        inc_t = load_list("inc_t", inc)
         sf_t = load_f32("sf_t", sf)
+        face_t = load_list("face_t", face)
         tail_t = load_list("tail_t", tail)
         head_t = load_list("head_t", head)
 
@@ -78,11 +78,8 @@ def tile_picked_yhodge_none_p_kernel(tc, x_words, x_scales, w1, w2, w3, sn, sa, 
             copy(g[:], raw[:].rearrange("p j n -> p n j"))
             return g
 
-        def pool_copy(dst, src):
-            nc.gpsimd.tensor_scalar(dst, src, 1.0, 0.0, MULT, ADD)
-
-        def quant(name, g):
-            codes = sb_pool.tile([P, N], U32, name=name + "_c", align_bytes=64)
+        def quant(name, g, tag):
+            codes = sb_pool.tile([P, N], U32, name=name + "_c", tag=tag, align_bytes=64)
             scales = sb_pool.tile([P, N], U8, name=name + "_s", align_bytes=64)
             nc.vector.quantize_mx(out=codes[:].bitcast(FP8X4), scales=scales[:], in_=g[:].rearrange("p n j -> p (n j)"))
             return codes, scales
@@ -94,11 +91,11 @@ def tile_picked_yhodge_none_p_kernel(tc, x_words, x_scales, w1, w2, w3, sn, sa, 
         w2_g = cast("w2_g", w2_raw, nc.vector.tensor_copy)
         gs = sb_pool.tile([P, S], U8, name="gs", align_bytes=64)
         nc.vector.tensor_copy(gs[:], xs[:].indirect(offs_t[:]))
-        w2_q = quant("w2_q", w2_g)
+        w2_q = quant("w2_q", w2_g, "w2_c")
 
-        w3_g = cast("w3_g", w3_raw, pool_copy)
+        w1_g = cast("w1_g", w1_raw, nc.scalar.copy)
         gw = sb_pool.tile([P, S], U32, name="gw", align_bytes=64)
-        h = sb_pool.tile([P, S], F32, name="h")
+        h = sb_pool.tile([P, S], F32, name="h", tag="w1_raw")
         y = sb_pool.tile([P, S], F32, name="y")
         for i in range(2):
             nc.vector.tensor_copy(half(gw, i), xw[:].indirect(half_list(offs_t, i)))
@@ -106,13 +103,13 @@ def tile_picked_yhodge_none_p_kernel(tc, x_words, x_scales, w1, w2, w3, sn, sa, 
             product(h_ps[:], w2_q, half(gw, i), half(gs, i))
             nc.scalar.copy(half(h, i), h_ps[:])
 
-        w1_g = cast("w1_g", w1_raw, nc.vector.tensor_copy)
-        w1_q = quant("w1_q", w1_g)
+        w3_g = cast("w3_g", w3_raw, nc.vector.tensor_copy)
+        w1_q = quant("w1_q", w1_g, "w1_c")
         y_ps = psum.tile([P, S], F32, name="y_ps")
         product(y_ps[:], w1_q, gw[:], gs[:])
         nc.scalar.copy(y[:], y_ps[:])
 
-        w3_q = quant("w3_q", w3_g)
+        w3_q = quant("w3_q", w3_g, "w1_g")
         own_ps = psum.tile([P, S], F32, name="own_ps")
         product(own_ps[:], w3_q, gw[:], gs[:])
 
@@ -137,5 +134,4 @@ def tile_picked_yhodge_none_p_kernel(tc, x_words, x_scales, w1, w2, w3, sn, sa, 
             nc.vector.tensor_tensor(half(c, i), dv[:].indirect(half_list(tail_t, i)), half(u, i), SUB)
         for i in range(2):
             nc.vector.tensor_tensor(half(res, i), dv[:].indirect(half_list(head_t, i)), half(c, i), SUB)
-            queue = nc.sync if i == 0 else nc.scalar
-            queue.dma_start(out[:, i * HALF : (i + 1) * HALF], half(res, i))
+            nc.sync.dma_start(out[:, i * HALF : (i + 1) * HALF], half(res, i))

@@ -1,6 +1,7 @@
 from contextlib import ExitStack
 
 import concourse.mybir as mybir
+from concourse.masks import make_identity
 
 K, T, S, N, V = 512, 2048, 512, 128, 256
 FLOPS = 3 * 2 * K * N * S
@@ -18,120 +19,169 @@ SUB = mybir.AluOpType.subtract
 
 P = 128
 PACK = 4
+QUADRANTS = 4
+QUADRANT_SIZE = P // QUADRANTS
+SCALE_ROWS = 4
+LIST_COL = 16
 HALF = S // 2
-LCOL = 16
+Y_PIECES = ((0, HALF), (HALF, HALF + P), (HALF + P, S))
 
 
-def tile_picked_yhodge_none_p_kernel(tc, x_words, x_scales, w1, w2, w3, sn, sa, sb, sf, offs, inc, head, tail, tri, trj, face, out):
+def tile_picked_yhodge_none_p_kernel(
+    tc, x_words, x_scales, w1, w2, w3, sn, sa, sb, sf, offs, inc, head, tail, tri, trj, face, out
+):
     nc = tc.nc
     with ExitStack() as ctx:
         lists = ctx.enter_context(tc.tile_pool(name="lists", bufs=1))
-        sb_pool = ctx.enter_context(tc.tile_pool(name="work", bufs=1))
+        work = ctx.enter_context(tc.tile_pool(name="work", bufs=1))
         psum = ctx.enter_context(tc.psum_pool(name="psum", bufs=1))
 
         def load_list(name, src):
-            t = lists.tile(list(src.shape), U16, name=name)
-            nc.sync.dma_start(t[:], src)
-            return t
+            tile = lists.tile(list(src.shape), U16, name=name)
+            nc.sync.dma_start(tile[:], src)
+            return tile
 
-        def load_f32(name, src):
-            t = sb_pool.tile(list(src.shape), F32, name=name)
-            nc.sync.dma_start(t[:], src)
-            return t
+        def load_signs(name, src):
+            tile = work.tile(list(src.shape), F32, name=name)
+            nc.sync.dma_start(tile[:], src)
+            return tile
 
-        def load_w(name, src):
-            t = sb_pool.tile([P, PACK, N], F32, name=name)
-            nc.sync.dma_start(t[:], src.rearrange("(p j) n -> p j n", j=PACK))
-            return t
+        def load_weight(name, src):
+            tile = work.tile([P, PACK, N], F32, name=name)
+            nc.sync.dma_start(tile[:], src.rearrange("(p j) n -> p j n", j=PACK))
+            return tile
 
-        def half_list(t, i):
-            return t[:, i * HALF // LCOL : (i + 1) * HALF // LCOL]
+        def round_weight(name, raw, copy):
+            grouped = work.tile([P, N, PACK], BF16, name=name, align_bytes=64)
+            copy(grouped[:], raw[:].rearrange("p j n -> p n j"))
+            return grouped
 
-        def half(t, i):
-            return t[:, i * HALF : (i + 1) * HALF]
-
-        xs = sb_pool.tile([P, T], U8, name="xs", align_bytes=64)
-        nc.vector.memset(xs[:].bitcast(I32), 0)
-        offs_t = load_list("offs_t", offs)
-        w2_raw = load_w("w2_raw", w2)
-        for q in range(4):
-            queue = nc.sync if q < 2 else nc.scalar
-            queue.dma_start(xs[32 * q : 32 * q + 4, :].bitcast(I32), x_scales[0, 4 * q : 4 * q + 4, :].bitcast(I32))
-        xw = sb_pool.tile([P, T], U32, name="xw", align_bytes=64)
-        nc.sync.dma_start(xw[:].bitcast(I32), x_words[0].rearrange("p n t -> p (n t)").bitcast(I32))
-        tri_t = load_list("tri_t", tri)
-        w1_raw = load_w("w1_raw", w1)
-        w3_raw = load_w("w3_raw", w3)
-        dv = sb_pool.tile([P, 2 * V], F32, name="dv")
-        nc.sync.dma_start(dv[:, :V], sa)
-        nc.sync.dma_start(dv[:, V:], sb)
-        trj_t = load_list("trj_t", trj)
-        cu = load_f32("cu", sn)
-        inc_t = load_list("inc_t", inc)
-        sf_t = load_f32("sf_t", sf)
-        face_t = load_list("face_t", face)
-        tail_t = load_list("tail_t", tail)
-        head_t = load_list("head_t", head)
-
-        def cast(name, raw, copy):
-            g = sb_pool.tile([P, N, PACK], BF16, name=name, align_bytes=64)
-            copy(g[:], raw[:].rearrange("p j n -> p n j"))
-            return g
-
-        def quant(name, g, tag):
-            codes = sb_pool.tile([P, N], U32, name=name + "_c", tag=tag, align_bytes=64)
-            scales = sb_pool.tile([P, N], U8, name=name + "_s", align_bytes=64)
-            nc.vector.quantize_mx(out=codes[:].bitcast(FP8X4), scales=scales[:], in_=g[:].rearrange("p n j -> p (n j)"))
+        def quantise(name, grouped, tag):
+            codes = work.tile([P, N], U32, name=name + "_codes", tag=tag, align_bytes=64)
+            scales = work.tile([P, N], U8, name=name + "_scales", align_bytes=64)
+            nc.vector.quantize_mx(
+                out=codes[:].bitcast(FP8X4), scales=scales[:], in_=grouped[:].rearrange("p n j -> p (n j)")
+            )
             return codes, scales
 
-        def product(dst, w, words, scales):
-            nc.tensor.matmul_mx(out=dst, lhsT=w[0][:].bitcast(FP8X4), lhsT_scale=w[1][:],
-                                rhs=words.bitcast(FP8X4), rhs_scale=scales, start=True, stop=True)
+        def product(dst, weight, words, scales):
+            w_codes, w_scales = weight
+            nc.tensor.matmul_mx(
+                out=dst,
+                lhsT=w_codes[:].bitcast(FP8X4),
+                lhsT_scale=w_scales[:],
+                rhs=words.bitcast(FP8X4),
+                rhs_scale=scales,
+                start=True,
+                stop=True,
+            )
 
-        w2_g = cast("w2_g", w2_raw, nc.vector.tensor_copy)
-        gs = sb_pool.tile([P, S], U8, name="gs", align_bytes=64)
-        nc.vector.tensor_copy(gs[:], xs[:].indirect(offs_t[:]))
-        w2_q = quant("w2_q", w2_g, "w2_c")
+        def half_list(tile, i):
+            return tile[:, i * HALF // LIST_COL : (i + 1) * HALF // LIST_COL]
 
-        w1_g = cast("w1_g", w1_raw, nc.scalar.copy)
-        gw = sb_pool.tile([P, S], U32, name="gw", align_bytes=64)
-        h = sb_pool.tile([P, S], F32, name="h", tag="w1_raw")
-        y = sb_pool.tile([P, S], F32, name="y")
+        def half(tile, i):
+            return tile[:, i * HALF : (i + 1) * HALF]
+
+        def square(tile, b):
+            return tile[:, b * P : (b + 1) * P]
+
+        xs = work.tile([P, T], U8, name="xs", align_bytes=64)
+        nc.vector.memset(xs[:].bitcast(I32), 0)
+        ident = work.tile([P, P], F32, name="ident")
+        nc.vector.memset(ident[:], 0.0)
+        make_identity(nc, ident[:], nomemset=True)
+
+        offs_t = load_list("offs_t", offs)
+        w1_raw = load_weight("w1_raw", w1)
+        for q in range(QUADRANTS):
+            queue = nc.sync if q < QUADRANTS // 2 else nc.scalar
+            queue.dma_start(
+                xs[QUADRANT_SIZE * q : QUADRANT_SIZE * q + SCALE_ROWS, :].bitcast(I32),
+                x_scales[0, SCALE_ROWS * q : SCALE_ROWS * (q + 1), :].bitcast(I32),
+            )
+        xw = work.tile([P, T], U32, name="xw", align_bytes=64)
+        nc.sync.dma_start(xw[:].bitcast(I32), x_words[0].rearrange("p n t -> p (n t)").bitcast(I32))
+        inc_t = load_list("inc_t", inc)
+        w2_raw = load_weight("w2_raw", w2)
+        w3_raw = load_weight("w3_raw", w3)
+        cu_win = load_signs("cu_win", sn)
+        dv_win = work.tile([P, 2 * V], F32, name="dv_win")
+        nc.sync.dma_start(dv_win[:, :V], sa)
+        nc.sync.dma_start(dv_win[:, V:], sb)
+        tri_t = load_list("tri_t", tri)
+        trj_t = load_list("trj_t", trj)
+        sf_t = load_signs("sf_t", sf)
+        tail_t = load_list("tail_t", tail)
+        head_t = load_list("head_t", head)
+        face_t = load_list("face_t", face)
+
+        w1_bf = round_weight("w1_bf", w1_raw, nc.vector.tensor_copy)
+        picked_scales = work.tile([P, S], U8, name="picked_scales", align_bytes=64)
+        nc.vector.tensor_copy(picked_scales[:], xs[:].indirect(offs_t[:]))
+        w1_q = quantise("w1", w1_bf, "w1_codes")
+
+        w2_bf = round_weight("w2_bf", w2_raw, nc.scalar.copy)
+        picked_words = work.tile([P, S], U32, name="picked_words", align_bytes=64)
+        y = work.tile([P, S], F32, name="y", tag="w2_raw")
         for i in range(2):
-            nc.vector.tensor_copy(half(gw, i), xw[:].indirect(half_list(offs_t, i)))
-            h_ps = psum.tile([P, HALF], F32, name="h_ps%d" % i)
-            product(h_ps[:], w2_q, half(gw, i), half(gs, i))
-            nc.scalar.copy(half(h, i), h_ps[:])
+            nc.vector.tensor_copy(half(picked_words, i), xw[:].indirect(half_list(offs_t, i)))
+        for piece, (lo, hi) in enumerate(Y_PIECES):
+            y_ps = psum.tile([P, hi - lo], F32, name="y_ps%d" % piece)
+            product(y_ps[:], w1_q, picked_words[:, lo:hi], picked_scales[:, lo:hi])
+            nc.scalar.copy(y[:, lo:hi], y_ps[:])
 
-        w3_g = cast("w3_g", w3_raw, nc.vector.tensor_copy)
-        w1_q = quant("w1_q", w1_g, "w1_c")
-        y_ps = psum.tile([P, S], F32, name="y_ps")
-        product(y_ps[:], w1_q, gw[:], gs[:])
-        nc.scalar.copy(y[:], y_ps[:])
+        w3_bf = round_weight("w3_bf", w3_raw, nc.vector.tensor_copy)
+        w2_q = quantise("w2", w2_bf, "w2_codes")
+        h = work.tile([P, S], F32, name="h")
+        h_ps = psum.tile([P, S], F32, name="h_ps")
+        product(h_ps[:], w2_q, picked_words[:], picked_scales[:])
+        nc.scalar.copy(h[:], h_ps[:])
 
-        w3_q = quant("w3_q", w3_g, "w1_g")
+        w3_q = quantise("w3", w3_bf, "w2_bf")
+        own = work.tile([P, S], F32, name="own")
         own_ps = psum.tile([P, S], F32, name="own_ps")
-        product(own_ps[:], w3_q, gw[:], gs[:])
+        product(own_ps[:], w3_q, picked_words[:], picked_scales[:])
+        nc.scalar.copy(own[:], own_ps[:])
 
-        ta = sb_pool.tile([P, V], F32, name="ta")
-        tb = sb_pool.tile([P, V], F32, name="tb")
-        li = sb_pool.tile([P, S], F32, name="li")
-        up = sb_pool.tile([P, S], F32, name="up")
-        u = sb_pool.tile([P, S], F32, name="u")
-        c = sb_pool.tile([P, S], F32, name="c")
-        res = sb_pool.tile([P, S], F32, name="res")
-        nc.vector.tensor_tensor(ta[:], h[:].indirect(tri_t[:]), dv[:, :V], MULT)
-        nc.vector.tensor_tensor(tb[:], h[:].indirect(trj_t[:]), dv[:, V:], MULT)
-        for i in (1, 0):
-            nc.vector.tensor_tensor(half(li, i), y[:].indirect(half_list(inc_t, i)), half(cu, i), MULT)
-        nc.vector.tensor_tensor(cu[:, :V], ta[:], tb[:], ADD)
-        nc.vector.tensor_tensor(dv[:, :V], li[:, 0::2], li[:, 1::2], ADD)
+        curl_a = work.tile([P, V], F32, name="curl_a")
+        curl_b = work.tile([P, V], F32, name="curl_b")
+        li = work.tile([P, S], F32, name="li")
+        up = work.tile([P, S], F32, name="up")
+        own_down = work.tile([P, S], F32, name="own_down")
+        result = work.tile([P, S], F32, name="result")
+        cu_turned = work.tile([P, V], F32, name="cu_turned")
+
         for i in range(2):
-            nc.vector.tensor_tensor(half(up, i), cu[:].indirect(half_list(face_t, i)), half(sf_t, i), MULT)
+            nc.vector.tensor_tensor(half(li, i), y[:].indirect(half_list(inc_t, i)), half(cu_win, i), MULT)
+        nc.vector.tensor_tensor(curl_a[:], h[:].indirect(tri_t[:]), dv_win[:, :V], MULT)
+        nc.vector.tensor_tensor(dv_win[:, :V], li[:, 0::2], li[:, 1::2], ADD)
+        nc.vector.tensor_tensor(curl_b[:], h[:].indirect(trj_t[:]), dv_win[:, V:], MULT)
+
+        squares = V // P
+        sum_ps = [psum.tile([P, P], F32, name="sum_ps%d" % b, tag="y_ps%d" % b) for b in range(squares)]
+        for e, term in enumerate((curl_a, curl_b)):
+            for b in range(squares):
+                nc.tensor.matmul(
+                    sum_ps[b][:], square(term, b), ident[:], start=(e == 0), stop=(e == 1), is_transpose=True
+                )
+        for b in range(squares):
+            nc.scalar.copy(square(cu_turned, b), sum_ps[b][:])
+        for b in range(squares):
+            back_ps = psum.tile([P, P], F32, name="back_ps%d" % b)
+            nc.tensor.transpose(back_ps[:], square(cu_turned, b), ident[:])
+            nc.scalar.copy(square(cu_win, b), back_ps[:])
+
+        tail_less_own = work.tile([P, S], F32, name="tail_less_own", tag="h")
         for i in range(2):
-            nc.vector.tensor_tensor(half(u, i), half(up, i), half(own_ps, i), ADD)
+            nc.vector.tensor_tensor(
+                half(tail_less_own, i), dv_win[:].indirect(half_list(tail_t, i)), half(own, i), SUB
+            )
         for i in range(2):
-            nc.vector.tensor_tensor(half(c, i), dv[:].indirect(half_list(tail_t, i)), half(u, i), SUB)
+            nc.vector.tensor_tensor(
+                half(own_down, i), dv_win[:].indirect(half_list(head_t, i)), half(tail_less_own, i), SUB
+            )
         for i in range(2):
-            nc.vector.tensor_tensor(half(res, i), dv[:].indirect(half_list(head_t, i)), half(c, i), SUB)
-            nc.sync.dma_start(out[:, i * HALF : (i + 1) * HALF], half(res, i))
+            nc.vector.tensor_tensor(half(up, i), cu_win[:].indirect(half_list(face_t, i)), half(sf_t, i), MULT)
+        for i in range(2):
+            nc.vector.tensor_tensor(half(result, i), half(up, i), half(own_down, i), ADD)
+            nc.sync.dma_start(half(out, i), half(result, i))

@@ -106,7 +106,7 @@ def tile_picked_yhodge_none_p_kernel(
         w3_raw = load_weight("w3_raw", w3)
         cu_win = load_signs("cu_win", sn)
         dv_win = work.tile([P, 2 * V], F32, name="dv_win")
-        nc.sync.dma_start(dv_win[:, :V], sa)
+        sa_t = load_signs("sa_t", sa)
         nc.sync.dma_start(dv_win[:, V:], sb)
         tri_t = load_list("tri_t", tri)
         trj_t = load_list("trj_t", trj)
@@ -153,7 +153,7 @@ def tile_picked_yhodge_none_p_kernel(
 
         for i in range(2):
             nc.vector.tensor_tensor(half(li, i), y[:].indirect(half_list(inc_t, i)), half(cu_win, i), MULT)
-        nc.vector.tensor_tensor(curl_a[:], h[:].indirect(tri_t[:]), dv_win[:, :V], MULT)
+        nc.vector.tensor_tensor(curl_a[:], h[:].indirect(tri_t[:]), sa_t[:], MULT)
         nc.vector.tensor_tensor(dv_win[:, :V], li[:, 0::2], li[:, 1::2], ADD)
         nc.vector.tensor_tensor(curl_b[:], h[:].indirect(trj_t[:]), dv_win[:, V:], MULT)
 
@@ -171,7 +171,7 @@ def tile_picked_yhodge_none_p_kernel(
             nc.tensor.transpose(back_ps[:], square(cu_turned, b), ident[:])
             nc.scalar.copy(square(cu_win, b), back_ps[:])
 
-        tail_less_own = work.tile([P, S], F32, name="tail_less_own", tag="h")
+        tail_less_own = work.tile([P, S], F32, name="tail_less_own")
         for i in range(2):
             nc.vector.tensor_tensor(
                 half(tail_less_own, i), dv_win[:].indirect(half_list(tail_t, i)), half(own, i), SUB

@@ -16,6 +16,7 @@ FP8X4 = mybir.dt.float8_e4m3fn_x4
 MULT = mybir.AluOpType.mult
 ADD = mybir.AluOpType.add
 SUB = mybir.AluOpType.subtract
+COPY = mybir.ActivationFunctionType.Copy
 
 P = 128
 PACK = 4
@@ -149,26 +150,33 @@ def tile_picked_yhodge_none_p_kernel(
         up = work.tile([P, S], F32, name="up")
         own_down = work.tile([P, S], F32, name="own_down")
         result = work.tile([P, S], F32, name="result")
-        cu_turned = work.tile([P, V], F32, name="cu_turned")
+        cu_turned = work.tile([P, 2 * V], F32, name="cu_turned")
 
         for i in range(2):
             nc.vector.tensor_tensor(half(li, i), y[:].indirect(half_list(inc_t, i)), half(cu_win, i), MULT)
-        nc.vector.tensor_tensor(curl_a[:], h[:].indirect(tri_t[:]), sa_t[:], MULT)
-        nc.vector.tensor_tensor(dv_win[:, :V], li[:, 0::2], li[:, 1::2], ADD)
-        nc.vector.tensor_tensor(curl_b[:], h[:].indirect(trj_t[:]), dv_win[:, V:], MULT)
+        nc.vector.tensor_copy(curl_a[:], h[:].indirect(tri_t[:]))
+        nc.gpsimd.tensor_tensor(dv_win[:, :V], li[:, 0::2], li[:, 1::2], ADD)
+        nc.vector.tensor_copy(curl_b[:], h[:].indirect(trj_t[:]))
 
         squares = V // P
-        sum_ps = [psum.tile([P, P], F32, name="sum_ps%d" % b, tag="y_ps%d" % b) for b in range(squares)]
+        sign_ps = psum.tile([P, 2 * squares, P], F32, name="sign_ps", tag="h_ps")
+        for e, signs in enumerate((sa_t[:], dv_win[:, V:])):
+            for b in range(squares):
+                nc.tensor.transpose(sign_ps[:, e * squares + b, :], square(signs, b), ident[:])
+        sign_cols = work.tile([P, 2 * squares], F32, name="sign_cols")
+        nc.scalar.copy(sign_cols[:], sign_ps[:, :, 0])
         for e, term in enumerate((curl_a, curl_b)):
             for b in range(squares):
-                nc.tensor.matmul(
-                    sum_ps[b][:], square(term, b), ident[:], start=(e == 0), stop=(e == 1), is_transpose=True
-                )
-        for b in range(squares):
-            nc.scalar.copy(square(cu_turned, b), sum_ps[b][:])
+                n = e * squares + b
+                term_ps = psum.tile([P, P], F32, name="term_ps%d" % n, tag=("y_ps0", "y_ps1", "y_ps2", "own_ps")[n])
+                nc.tensor.transpose(term_ps[:], square(term, b), ident[:])
+                nc.scalar.activation(square(cu_turned, n), term_ps[:], COPY, scale=sign_cols[:, n : n + 1])
         for b in range(squares):
             back_ps = psum.tile([P, P], F32, name="back_ps%d" % b)
-            nc.tensor.transpose(back_ps[:], square(cu_turned, b), ident[:])
+            for e in range(2):
+                nc.tensor.matmul(
+                    back_ps[:], square(cu_turned, e * squares + b), ident[:], start=(e == 0), stop=(e == 1), is_transpose=True
+                )
             nc.scalar.copy(square(cu_win, b), back_ps[:])
 
         tail_less_own = work.tile([P, S], F32, name="tail_less_own")

@@ -25,6 +25,7 @@ QUADRANT_SIZE = P // QUADRANTS
 SCALE_ROWS = 4
 LIST_COL = 16
 HALF = S // 2
+GPSIMD_CLEARS = 320
 Y_PIECES = ((0, HALF), (HALF, HALF + P), (HALF + P, S))
 
 
@@ -87,13 +88,15 @@ def tile_picked_yhodge_none_p_kernel(
             return tile[:, b * P : (b + 1) * P]
 
         xs = work.tile([P, T], U8, name="xs", align_bytes=64)
-        nc.vector.memset(xs[:].bitcast(I32), 0)
+        xs_words = xs[:].bitcast(I32)
+        nc.gpsimd.memset(xs_words[:, :GPSIMD_CLEARS], 0)
+        nc.vector.memset(xs_words[:, GPSIMD_CLEARS:], 0)
         ident = work.tile([P, P], F32, name="ident")
         nc.vector.memset(ident[:], 0.0)
         make_identity(nc, ident[:], nomemset=True)
 
-        offs_t = load_list("offs_t", offs)
         w1_raw = load_weight("w1_raw", w1)
+        offs_t = load_list("offs_t", offs)
         for q in range(QUADRANTS):
             queue = nc.sync if q < QUADRANTS // 2 else nc.scalar
             queue.dma_start(

@@ -25,7 +25,7 @@ QUADRANT_SIZE = P // QUADRANTS
 SCALE_ROWS = 4
 LIST_COL = 16
 HALF = S // 2
-GPSIMD_CLEARS = 320
+GPSIMD_CLEARS = 384
 Y_PIECES = ((0, HALF), (HALF, HALF + P), (HALF + P, S))
 
 
@@ -137,9 +137,10 @@ def tile_picked_yhodge_none_p_kernel(
         w3_bf = round_weight("w3_bf", w3_raw, nc.vector.tensor_copy)
         w2_q = quantise("w2", w2_bf, "w2_codes")
         h = work.tile([P, S], F32, name="h")
-        h_ps = psum.tile([P, S], F32, name="h_ps")
-        product(h_ps[:], w2_q, picked_words[:], picked_scales[:])
-        nc.scalar.copy(h[:], h_ps[:])
+        for i in range(2):
+            h_ps = psum.tile([P, HALF], F32, name="h_ps%d" % i)
+            product(h_ps[:], w2_q, half(picked_words, i), half(picked_scales, i))
+            nc.scalar.copy(half(h, i), h_ps[:])
 
         w3_q = quantise("w3", w3_bf, "w2_bf")
         own = work.tile([P, S], F32, name="own")
@@ -158,11 +159,13 @@ def tile_picked_yhodge_none_p_kernel(
         for i in range(2):
             nc.vector.tensor_tensor(half(li, i), y[:].indirect(half_list(inc_t, i)), half(cu_win, i), MULT)
         nc.vector.tensor_copy(curl_a[:], h[:].indirect(tri_t[:]))
-        nc.gpsimd.tensor_tensor(dv_win[:, :V], li[:, 0::2], li[:, 1::2], ADD)
+        for i in range(2):
+            pairs = half(li, i)
+            nc.gpsimd.tensor_tensor(square(dv_win, i), pairs[:, 0::2], pairs[:, 1::2], ADD)
         nc.vector.tensor_copy(curl_b[:], h[:].indirect(trj_t[:]))
 
         squares = V // P
-        sign_ps = psum.tile([P, 2 * squares, P], F32, name="sign_ps", tag="h_ps")
+        sign_ps = psum.tile([P, 2 * squares, P], F32, name="sign_ps", tag="h_ps0")
         for e, signs in enumerate((sa_t[:], dv_win[:, V:])):
             for b in range(squares):
                 nc.tensor.transpose(sign_ps[:, e * squares + b, :], square(signs, b), ident[:])

@@ -124,7 +124,10 @@ def tile_picked_yhodge_none_p_kernel(
         nc.vector.tensor_copy(picked_scales[:], xs[:].indirect(offs_t[:]))
         w1_q = quantise("w1", w1_bf, "w1_codes")
 
-        w2_bf = round_weight("w2_bf", w2_raw, nc.scalar.copy)
+        w2_bf = work.tile([P, N, PACK], BF16, name="w2_bf", align_bytes=64)
+        w2_cols = w2_raw[:].rearrange("p j n -> p n j")
+        nc.scalar.copy(w2_bf[:, : N // 2, :], w2_cols[:, : N // 2, :])
+        nc.gpsimd.tensor_copy(w2_bf[:, N // 2 :, :], w2_cols[:, N // 2 :, :])
         picked_words = work.tile([P, S], U32, name="picked_words", align_bytes=64)
         y = work.tile([P, S], F32, name="y", tag="w2_raw")
         for i in range(2):
@@ -194,8 +197,9 @@ def tile_picked_yhodge_none_p_kernel(
             nc.vector.tensor_tensor(
                 half(own_down, i), dv_win[:].indirect(half_list(head_t, i)), half(tail_less_own, i), SUB
             )
-        for i in range(2):
-            nc.vector.tensor_tensor(half(up, i), cu_win[:].indirect(half_list(face_t, i)), half(sf_t, i), MULT)
-        for i in range(2):
-            nc.vector.tensor_tensor(half(result, i), half(up, i), half(own_down, i), ADD)
-            nc.sync.dma_start(half(out, i), half(result, i))
+        for lo, hi in Y_PIECES:
+            offsets = face_t[:, lo // LIST_COL : hi // LIST_COL]
+            nc.vector.tensor_tensor(up[:, lo:hi], cu_win[:].indirect(offsets), sf_t[:, lo:hi], MULT)
+        for lo, hi in Y_PIECES:
+            nc.vector.tensor_tensor(result[:, lo:hi], up[:, lo:hi], own_down[:, lo:hi], ADD)
+            nc.sync.dma_start(out[:, lo:hi], result[:, lo:hi])

@@ -97,11 +97,11 @@ def tile_picked_yhodge_none_p_kernel(
 
         w1_raw = load_weight("w1_raw", w1)
         offs_t = load_list("offs_t", offs)
-        for q in range(QUADRANTS):
-            queue = nc.sync if q < QUADRANTS // 2 else nc.scalar
+        for r in range(SCALE_ROWS):
+            queue = nc.sync if r < SCALE_ROWS // 2 else nc.scalar
             queue.dma_start(
-                xs[QUADRANT_SIZE * q : QUADRANT_SIZE * q + SCALE_ROWS, :].bitcast(I32),
-                x_scales[0, SCALE_ROWS * q : SCALE_ROWS * (q + 1), :].bitcast(I32),
+                xs[r:P:QUADRANT_SIZE, :].bitcast(I32),
+                x_scales[0, r : QUADRANTS * SCALE_ROWS : SCALE_ROWS, :].bitcast(I32),
             )
         xw = work.tile([P, T], U32, name="xw", align_bytes=64)
         nc.sync.dma_start(xw[:].bitcast(I32), x_words[0].rearrange("p n t -> p (n t)").bitcast(I32))

@@ -25,7 +25,6 @@ QUADRANT_SIZE = P // QUADRANTS
 SCALE_ROWS = 4
 LIST_COL = 16
 HALF = S // 2
-GPSIMD_CLEARS = 384
 Y_PIECES = ((0, HALF), (HALF, HALF + P), (HALF + P, S))
 
 
@@ -89,11 +88,9 @@ def tile_picked_yhodge_none_p_kernel(
 
         xs = work.tile([P, T], U8, name="xs", align_bytes=64)
         xs_words = xs[:].bitcast(I32)
-        nc.gpsimd.memset(xs_words[:, :GPSIMD_CLEARS], 0)
-        nc.vector.memset(xs_words[:, GPSIMD_CLEARS:], 0)
+        nc.vector.memset(xs_words, 0)
         ident = work.tile([P, P], F32, name="ident")
-        nc.vector.memset(ident[:], 0.0)
-        make_identity(nc, ident[:], nomemset=True)
+        make_identity(nc, ident[:])
 
         w1_raw = load_weight("w1_raw", w1)
         offs_t = load_list("offs_t", offs)

@@ -44,7 +44,8 @@ def tile_picked_yhodge_none_p_kernel(
 
         def load_signs(name, src):
             tile = work.tile(list(src.shape), F32, name=name)
-            nc.sync.dma_start(tile[:], src)
+            for lo in range(0, src.shape[1], HALF):
+                nc.sync.dma_start(tile[:, lo : lo + HALF], src[:, lo : lo + HALF])
             return tile
 
         def load_weight(name, src):

@@ -23,6 +23,7 @@ PACK = 4
 QUADRANTS = 4
 QUADRANT_SIZE = P // QUADRANTS
 SCALE_ROWS = 4
+SCALE_START = 12
 LIST_COL = 16
 HALF = S // 2
 Y_PIECES = ((0, HALF), (HALF, HALF + P), (HALF + P, S))
@@ -98,7 +99,7 @@ def tile_picked_yhodge_none_p_kernel(
         for r in range(SCALE_ROWS):
             queue = nc.sync if r < SCALE_ROWS // 2 else nc.scalar
             queue.dma_start(
-                xs[r:P:QUADRANT_SIZE, :].bitcast(I32),
+                xs[SCALE_START + r : P : QUADRANT_SIZE, :].bitcast(I32),
                 x_scales[0, r : QUADRANTS * SCALE_ROWS : SCALE_ROWS, :].bitcast(I32),
             )
         xw = work.tile([P, T], U32, name="xw", align_bytes=64)
@@ -132,7 +133,7 @@ def tile_picked_yhodge_none_p_kernel(
             nc.vector.tensor_copy(half(picked_words, i), xw[:].indirect(half_list(offs_t, i)))
         for piece, (lo, hi) in enumerate(Y_PIECES):
             y_ps = psum.tile([P, hi - lo], F32, name="y_ps%d" % piece)
-            product(y_ps[:], w1_q, picked_words[:, lo:hi], picked_scales[:, lo:hi])
+            product(y_ps[:], w1_q, picked_words[:, lo:hi], picked_scales[SCALE_START:, lo:hi])
             nc.scalar.copy(y[:, lo:hi], y_ps[:])
 
         w3_bf = round_weight("w3_bf", w3_raw, nc.vector.tensor_copy)
@@ -140,13 +141,13 @@ def tile_picked_yhodge_none_p_kernel(
         h = work.tile([P, S], F32, name="h")
         for i in range(2):
             h_ps = psum.tile([P, HALF], F32, name="h_ps%d" % i)
-            product(h_ps[:], w2_q, half(picked_words, i), half(picked_scales, i))
+            product(h_ps[:], w2_q, half(picked_words, i), picked_scales[SCALE_START:, i * HALF : (i + 1) * HALF])
             nc.scalar.copy(half(h, i), h_ps[:])
 
         w3_q = quantise("w3", w3_bf, "w2_bf")
         own = work.tile([P, S], F32, name="own")
         own_ps = psum.tile([P, S], F32, name="own_ps")
-        product(own_ps[:], w3_q, picked_words[:], picked_scales[:])
+        product(own_ps[:], w3_q, picked_words[:], picked_scales[SCALE_START:, :])
         nc.scalar.copy(own[:], own_ps[:])
 
         curl_a = work.tile([P, V], F32, name="curl_a")

@@ -196,7 +196,7 @@ def tile_picked_yhodge_none_p_kernel(
             nc.vector.tensor_tensor(
                 half(own_down, i), dv_win[:].indirect(half_list(head_t, i)), half(tail_less_own, i), SUB
             )
-        for lo, hi in Y_PIECES:
+        for lo, hi in ((0, S - P), (S - P, S)):
             offsets = face_t[:, lo // LIST_COL : hi // LIST_COL]
             nc.vector.tensor_tensor(up[:, lo:hi], cu_win[:].indirect(offsets), sf_t[:, lo:hi], MULT)
         for lo, hi in Y_PIECES:

@@ -1,7 +1,6 @@
 from contextlib import ExitStack
 
 import concourse.mybir as mybir
-from concourse.masks import make_identity
 
 K, T, S, N, V = 512, 2048, 512, 128, 256
 FLOPS = 3 * 2 * K * N * S
@@ -45,8 +44,7 @@ def tile_picked_yhodge_none_p_kernel(
 
         def load_signs(name, src):
             tile = work.tile(list(src.shape), F32, name=name)
-            for lo in range(0, src.shape[1], HALF):
-                nc.sync.dma_start(tile[:, lo : lo + HALF], src[:, lo : lo + HALF])
+            nc.sync.dma_start(tile[:], src)
             return tile
 
         def load_weight(name, src):
@@ -79,20 +77,17 @@ def tile_picked_yhodge_none_p_kernel(
                 stop=True,
             )
 
+        def entries(tile, lo, hi):
+            return tile[:, lo // LIST_COL : hi // LIST_COL]
+
         def half_list(tile, i):
-            return tile[:, i * HALF // LIST_COL : (i + 1) * HALF // LIST_COL]
+            return entries(tile, i * HALF, (i + 1) * HALF)
 
         def half(tile, i):
             return tile[:, i * HALF : (i + 1) * HALF]
 
-        def square(tile, b):
-            return tile[:, b * P : (b + 1) * P]
-
         xs = work.tile([P, T], U8, name="xs", align_bytes=64)
-        xs_words = xs[:].bitcast(I32)
-        nc.vector.memset(xs_words, 0)
-        ident = work.tile([P, P], F32, name="ident")
-        make_identity(nc, ident[:])
+        nc.vector.memset(xs[:].bitcast(I32), 0)
 
         w1_raw = load_weight("w1_raw", w1)
         offs_t = load_list("offs_t", offs)
@@ -109,14 +104,14 @@ def tile_picked_yhodge_none_p_kernel(
         w3_raw = load_weight("w3_raw", w3)
         cu_win = load_signs("cu_win", sn)
         dv_win = work.tile([P, 2 * V], F32, name="dv_win")
-        sa_t = load_signs("sa_t", sa)
-        nc.sync.dma_start(dv_win[:, V:], sb)
         tri_t = load_list("tri_t", tri)
         trj_t = load_list("trj_t", trj)
-        sf_t = load_signs("sf_t", sf)
+        sa_t = load_signs("sa_t", sa)
+        nc.sync.dma_start(dv_win[:, V:], sb)
         tail_t = load_list("tail_t", tail)
         head_t = load_list("head_t", head)
         face_t = load_list("face_t", face)
+        sf_t = load_signs("sf_t", sf)
 
         w1_bf = round_weight("w1_bf", w1_raw, nc.vector.tensor_copy)
         picked_scales = work.tile([P, S], U8, name="picked_scales", align_bytes=64)
@@ -129,15 +124,15 @@ def tile_picked_yhodge_none_p_kernel(
         nc.gpsimd.tensor_copy(w2_bf[:, N // 2 :, :], w2_cols[:, N // 2 :, :])
         picked_words = work.tile([P, S], U32, name="picked_words", align_bytes=64)
         y = work.tile([P, S], F32, name="y", tag="w2_raw")
-        for i in range(2):
-            nc.vector.tensor_copy(half(picked_words, i), xw[:].indirect(half_list(offs_t, i)))
+        for lo, hi in Y_PIECES:
+            nc.vector.tensor_copy(picked_words[:, lo:hi], xw[:].indirect(entries(offs_t, lo, hi)))
         for piece, (lo, hi) in enumerate(Y_PIECES):
             y_ps = psum.tile([P, hi - lo], F32, name="y_ps%d" % piece)
             product(y_ps[:], w1_q, picked_words[:, lo:hi], picked_scales[SCALE_START:, lo:hi])
             nc.scalar.copy(y[:, lo:hi], y_ps[:])
 
-        w3_bf = round_weight("w3_bf", w3_raw, nc.vector.tensor_copy)
         w2_q = quantise("w2", w2_bf, "w2_codes")
+        w3_bf = round_weight("w3_bf", w3_raw, nc.vector.tensor_copy)
         h = work.tile([P, S], F32, name="h")
         for i in range(2):
             h_ps = psum.tile([P, HALF], F32, name="h_ps%d" % i)
@@ -145,60 +140,41 @@ def tile_picked_yhodge_none_p_kernel(
             nc.scalar.copy(half(h, i), h_ps[:])
 
         w3_q = quantise("w3", w3_bf, "w2_bf")
-        own = work.tile([P, S], F32, name="own")
         own_ps = psum.tile([P, S], F32, name="own_ps")
         product(own_ps[:], w3_q, picked_words[:], picked_scales[SCALE_START:, :])
-        nc.scalar.copy(own[:], own_ps[:])
 
         curl_a = work.tile([P, V], F32, name="curl_a")
         curl_b = work.tile([P, V], F32, name="curl_b")
+        term_a = work.tile([P, V], F32, name="term_a")
+        term_b = work.tile([P, V], F32, name="term_b")
         li = work.tile([P, S], F32, name="li")
+        at_tail = work.tile([P, S], F32, name="at_tail")
+        at_face = work.tile([P, S], F32, name="at_face")
         up = work.tile([P, S], F32, name="up")
-        own_down = work.tile([P, S], F32, name="own_down")
+        down = work.tile([P, S], F32, name="down")
+        rest = work.tile([P, S], F32, name="rest")
         result = work.tile([P, S], F32, name="result")
-        cu_turned = work.tile([P, 2 * V], F32, name="cu_turned")
 
         for i in range(2):
             nc.vector.tensor_tensor(half(li, i), y[:].indirect(half_list(inc_t, i)), half(cu_win, i), MULT)
-        nc.vector.tensor_copy(curl_a[:], h[:].indirect(tri_t[:]))
+        nc.scalar.activation(curl_a[:], h[:].indirect(tri_t[:]), COPY)
+        nc.scalar.activation(curl_b[:], h[:].indirect(trj_t[:]), COPY)
         for i in range(2):
             pairs = half(li, i)
-            nc.gpsimd.tensor_tensor(square(dv_win, i), pairs[:, 0::2], pairs[:, 1::2], ADD)
-        nc.vector.tensor_copy(curl_b[:], h[:].indirect(trj_t[:]))
-
-        squares = V // P
-        sign_ps = psum.tile([P, 2 * squares, P], F32, name="sign_ps", tag="h_ps0")
-        for e, signs in enumerate((sa_t[:], dv_win[:, V:])):
-            for b in range(squares):
-                nc.tensor.transpose(sign_ps[:, e * squares + b, :], square(signs, b), ident[:])
-        sign_cols = work.tile([P, 2 * squares], F32, name="sign_cols")
-        nc.scalar.copy(sign_cols[:], sign_ps[:, :, 0])
-        for e, term in enumerate((curl_a, curl_b)):
-            for b in range(squares):
-                n = e * squares + b
-                term_ps = psum.tile([P, P], F32, name="term_ps%d" % n, tag=("y_ps0", "y_ps1", "y_ps2", "own_ps")[n])
-                nc.tensor.transpose(term_ps[:], square(term, b), ident[:])
-                nc.scalar.activation(square(cu_turned, n), term_ps[:], COPY, scale=sign_cols[:, n : n + 1])
-        for b in range(squares):
-            back_ps = psum.tile([P, P], F32, name="back_ps%d" % b)
-            for e in range(2):
-                nc.tensor.matmul(
-                    back_ps[:], square(cu_turned, e * squares + b), ident[:], start=(e == 0), stop=(e == 1), is_transpose=True
-                )
-            nc.scalar.copy(square(cu_win, b), back_ps[:])
-
-        tail_less_own = work.tile([P, S], F32, name="tail_less_own")
+            nc.vector.tensor_tensor(dv_win[:, i * P : (i + 1) * P], pairs[:, 0::2], pairs[:, 1::2], ADD)
+        nc.vector.tensor_tensor(term_a[:], curl_a[:], sa_t[:], MULT)
+        nc.vector.tensor_tensor(term_b[:], curl_b[:], dv_win[:, V:], MULT)
         for i in range(2):
-            nc.vector.tensor_tensor(
-                half(tail_less_own, i), dv_win[:].indirect(half_list(tail_t, i)), half(own, i), SUB
-            )
+            nc.scalar.activation(half(at_tail, i), dv_win[:].indirect(half_list(tail_t, i)), COPY)
+        nc.vector.tensor_tensor(cu_win[:, :V], term_a[:], term_b[:], ADD)
         for i in range(2):
-            nc.vector.tensor_tensor(
-                half(own_down, i), dv_win[:].indirect(half_list(head_t, i)), half(tail_less_own, i), SUB
-            )
-        for lo, hi in ((0, S - P), (S - P, S)):
-            offsets = face_t[:, lo // LIST_COL : hi // LIST_COL]
-            nc.vector.tensor_tensor(up[:, lo:hi], cu_win[:].indirect(offsets), sf_t[:, lo:hi], MULT)
+            nc.scalar.activation(half(at_face, i), cu_win[:].indirect(half_list(face_t, i)), COPY)
+        for i in range(2):
+            nc.vector.tensor_tensor(half(down, i), dv_win[:].indirect(half_list(head_t, i)), half(at_tail, i), SUB)
+        for i in range(2):
+            nc.vector.tensor_tensor(half(rest, i), half(own_ps, i), half(down, i), ADD)
+        for i in range(2):
+            nc.vector.tensor_tensor(half(up, i), half(at_face, i), half(sf_t, i), MULT)
         for lo, hi in Y_PIECES:
-            nc.vector.tensor_tensor(result[:, lo:hi], up[:, lo:hi], own_down[:, lo:hi], ADD)
+            nc.vector.tensor_tensor(result[:, lo:hi], rest[:, lo:hi], up[:, lo:hi], ADD)
             nc.sync.dma_start(out[:, lo:hi], result[:, lo:hi])

@@ -106,12 +106,12 @@ def tile_picked_yhodge_none_p_kernel(
         dv_win = work.tile([P, 2 * V], F32, name="dv_win")
         tri_t = load_list("tri_t", tri)
         trj_t = load_list("trj_t", trj)
-        sa_t = load_signs("sa_t", sa)
-        nc.sync.dma_start(dv_win[:, V:], sb)
-        tail_t = load_list("tail_t", tail)
-        head_t = load_list("head_t", head)
-        face_t = load_list("face_t", face)
+        sb_t = load_signs("sb_t", sb)
+        nc.sync.dma_start(dv_win[:, V:], sa)
         sf_t = load_signs("sf_t", sf)
+        head_t = load_list("head_t", head)
+        tail_t = load_list("tail_t", tail)
+        face_t = load_list("face_t", face)
 
         w1_bf = round_weight("w1_bf", w1_raw, nc.vector.tensor_copy)
         picked_scales = work.tile([P, S], U8, name="picked_scales", align_bytes=64)
@@ -144,12 +144,12 @@ def tile_picked_yhodge_none_p_kernel(
         product(own_ps[:], w3_q, picked_words[:], picked_scales[SCALE_START:, :])
 
         curl_a = work.tile([P, V], F32, name="curl_a")
-        curl_b = work.tile([P, V], F32, name="curl_b")
+        curl_b = work.tile([P, P], F32, name="curl_b")
         term_a = work.tile([P, V], F32, name="term_a")
         term_b = work.tile([P, V], F32, name="term_b")
         li = work.tile([P, S], F32, name="li")
-        at_tail = work.tile([P, S], F32, name="at_tail")
-        at_face = work.tile([P, S], F32, name="at_face")
+        at_tail = [work.tile([P, HALF], F32, name="at_tail%d" % i) for i in range(2)]
+        at_face = work.tile([P, HALF], F32, name="at_face")
         up = work.tile([P, S], F32, name="up")
         down = work.tile([P, S], F32, name="down")
         rest = work.tile([P, S], F32, name="rest")
@@ -158,23 +158,31 @@ def tile_picked_yhodge_none_p_kernel(
         for i in range(2):
             nc.vector.tensor_tensor(half(li, i), y[:].indirect(half_list(inc_t, i)), half(cu_win, i), MULT)
         nc.scalar.activation(curl_a[:], h[:].indirect(tri_t[:]), COPY)
-        nc.scalar.activation(curl_b[:], h[:].indirect(trj_t[:]), COPY)
+        nc.scalar.activation(curl_b[:], h[:].indirect(entries(trj_t, P, V)), COPY)
         for i in range(2):
             pairs = half(li, i)
             nc.vector.tensor_tensor(dv_win[:, i * P : (i + 1) * P], pairs[:, 0::2], pairs[:, 1::2], ADD)
-        nc.vector.tensor_tensor(term_a[:], curl_a[:], sa_t[:], MULT)
-        nc.vector.tensor_tensor(term_b[:], curl_b[:], dv_win[:, V:], MULT)
+        nc.vector.tensor_tensor(term_b[:, :P], h[:].indirect(entries(trj_t, 0, P)), sb_t[:, :P], MULT)
+        nc.vector.tensor_tensor(term_a[:], curl_a[:], dv_win[:, V:], MULT)
+        nc.vector.tensor_tensor(term_b[:, P:], curl_b[:], sb_t[:, P:], MULT)
         for i in range(2):
-            nc.scalar.activation(half(at_tail, i), dv_win[:].indirect(half_list(tail_t, i)), COPY)
-        nc.vector.tensor_tensor(cu_win[:, :V], term_a[:], term_b[:], ADD)
+            nc.scalar.activation(at_tail[i][:], dv_win[:].indirect(half_list(tail_t, i)), COPY)
         for i in range(2):
-            nc.scalar.activation(half(at_face, i), cu_win[:].indirect(half_list(face_t, i)), COPY)
-        for i in range(2):
-            nc.vector.tensor_tensor(half(down, i), dv_win[:].indirect(half_list(head_t, i)), half(at_tail, i), SUB)
-        for i in range(2):
-            nc.vector.tensor_tensor(half(rest, i), half(own_ps, i), half(down, i), ADD)
-        for i in range(2):
-            nc.vector.tensor_tensor(half(up, i), half(at_face, i), half(sf_t, i), MULT)
-        for lo, hi in Y_PIECES:
-            nc.vector.tensor_tensor(result[:, lo:hi], rest[:, lo:hi], up[:, lo:hi], ADD)
+            cols = slice(i * P, (i + 1) * P)
+            nc.vector.tensor_tensor(cu_win[:, cols], term_a[:, cols], term_b[:, cols], ADD)
+        nc.scalar.activation(at_face[:], cu_win[:].indirect(half_list(face_t, 1)), COPY)
+        nc.vector.tensor_tensor(half(up, 0), cu_win[:].indirect(half_list(face_t, 0)), half(sf_t, 0), MULT)
+        nc.vector.tensor_tensor(half(down, 0), dv_win[:].indirect(half_list(head_t, 0)), at_tail[0][:], SUB)
+        at_head = work.tile([P, HALF], F32, name="at_head", tag="at_tail0")
+        for lo, hi in Y_PIECES[1:]:
+            nc.scalar.activation(at_head[:, lo - HALF : hi - HALF], dv_win[:].indirect(entries(head_t, lo, hi)), COPY)
+        nc.vector.tensor_tensor(half(down, 1), half(own_ps, 1), at_tail[1][:], SUB)
+        nc.vector.tensor_tensor(half(rest, 0), half(own_ps, 0), half(down, 0), ADD)
+        nc.vector.tensor_tensor(half(up, 1), at_face[:], half(sf_t, 1), MULT)
+        nc.vector.tensor_tensor(half(result, 0), half(rest, 0), half(up, 0), ADD)
+        nc.sync.dma_start(half(out, 0), half(result, 0))
+        for lo, hi in Y_PIECES[1:]:
+            nc.vector.tensor_tensor(rest[:, lo:hi], down[:, lo:hi], up[:, lo:hi], ADD)
+        for lo, hi in Y_PIECES[1:]:
+            nc.vector.tensor_tensor(result[:, lo:hi], rest[:, lo:hi], at_head[:, lo - HALF : hi - HALF], ADD)
             nc.sync.dma_start(out[:, lo:hi], result[:, lo:hi])

@@ -118,10 +118,7 @@ def tile_picked_yhodge_none_p_kernel(
         nc.vector.tensor_copy(picked_scales[:], xs[:].indirect(offs_t[:]))
         w1_q = quantise("w1", w1_bf, "w1_codes")
 
-        w2_bf = work.tile([P, N, PACK], BF16, name="w2_bf", align_bytes=64)
-        w2_cols = w2_raw[:].rearrange("p j n -> p n j")
-        nc.scalar.copy(w2_bf[:, : N // 2, :], w2_cols[:, : N // 2, :])
-        nc.gpsimd.tensor_copy(w2_bf[:, N // 2 :, :], w2_cols[:, N // 2 :, :])
+        w2_bf = round_weight("w2_bf", w2_raw, nc.scalar.copy)
         picked_words = work.tile([P, S], U32, name="picked_words", align_bytes=64)
         y = work.tile([P, S], F32, name="y", tag="w2_raw")
         for lo, hi in Y_PIECES:
@@ -134,10 +131,10 @@ def tile_picked_yhodge_none_p_kernel(
         w2_q = quantise("w2", w2_bf, "w2_codes")
         w3_bf = round_weight("w3_bf", w3_raw, nc.vector.tensor_copy)
         h = work.tile([P, S], F32, name="h")
-        for i in range(2):
-            h_ps = psum.tile([P, HALF], F32, name="h_ps%d" % i)
-            product(h_ps[:], w2_q, half(picked_words, i), picked_scales[SCALE_START:, i * HALF : (i + 1) * HALF])
-            nc.scalar.copy(half(h, i), h_ps[:])
+        for piece, (lo, hi) in enumerate(Y_PIECES):
+            h_ps = psum.tile([P, hi - lo], F32, name="h_ps%d" % piece)
+            product(h_ps[:], w2_q, picked_words[:, lo:hi], picked_scales[SCALE_START:, lo:hi])
+            nc.scalar.copy(h[:, lo:hi], h_ps[:])
 
         w3_q = quantise("w3", w3_bf, "w2_bf")
         own_ps = psum.tile([P, S], F32, name="own_ps")

@@ -99,17 +99,22 @@ def tile_picked_yhodge_none_p_kernel(
             )
         xw = work.tile([P, T], U32, name="xw", align_bytes=64)
         nc.sync.dma_start(xw[:].bitcast(I32), x_words[0].rearrange("p n t -> p (n t)").bitcast(I32))
-        inc_t = load_list("inc_t", inc)
         w2_raw = load_weight("w2_raw", w2)
-        w3_raw = load_weight("w3_raw", w3)
-        cu_win = load_signs("cu_win", sn)
-        dv_win = work.tile([P, 2 * V], F32, name="dv_win")
-        tri_t = load_list("tri_t", tri)
         trj_t = load_list("trj_t", trj)
+        tri_t = load_list("tri_t", tri)
         sb_t = load_signs("sb_t", sb)
+        w3_raw = load_weight("w3_raw", w3)
+        sn_first = work.tile([P, HALF], F32, name="sn_first")
+        nc.sync.dma_start(sn_first[:], half(sn, 0))
+        cu_win = work.tile([P, 2 * V], F32, name="cu_win")
+        nc.sync.dma_start(cu_win[:, V:], half(sn, 1))
+        inc_t = load_list("inc_t", inc)
+        dv_win = work.tile([P, 2 * V], F32, name="dv_win")
         nc.sync.dma_start(dv_win[:, V:], sa)
-        sf_t = load_signs("sf_t", sf)
         head_t = load_list("head_t", head)
+        sf_t = work.tile([P, S], F32, name="sf_t")
+        for i in range(2):
+            nc.sync.dma_start(half(sf_t, i), half(sf, i))
         tail_t = load_list("tail_t", tail)
         face_t = load_list("face_t", face)
 
@@ -137,49 +142,42 @@ def tile_picked_yhodge_none_p_kernel(
             nc.scalar.copy(h[:, lo:hi], h_ps[:])
 
         w3_q = quantise("w3", w3_bf, "w2_bf")
-        own_ps = psum.tile([P, S], F32, name="own_ps")
-        product(own_ps[:], w3_q, picked_words[:], picked_scales[SCALE_START:, :])
-
         curl_a = work.tile([P, V], F32, name="curl_a")
-        curl_b = work.tile([P, P], F32, name="curl_b")
-        term_a = work.tile([P, V], F32, name="term_a")
-        term_b = work.tile([P, V], F32, name="term_b")
-        li = work.tile([P, S], F32, name="li")
-        at_tail = [work.tile([P, HALF], F32, name="at_tail%d" % i) for i in range(2)]
-        at_face = work.tile([P, HALF], F32, name="at_face")
-        up = work.tile([P, S], F32, name="up")
-        down = work.tile([P, S], F32, name="down")
-        rest = work.tile([P, S], F32, name="rest")
-        result = work.tile([P, S], F32, name="result")
-
-        for i in range(2):
-            nc.vector.tensor_tensor(half(li, i), y[:].indirect(half_list(inc_t, i)), half(cu_win, i), MULT)
         nc.scalar.activation(curl_a[:], h[:].indirect(tri_t[:]), COPY)
-        nc.scalar.activation(curl_b[:], h[:].indirect(entries(trj_t, P, V)), COPY)
+        own = work.tile([P, S], F32, name="own")
+        for i in range(2):
+            own_ps = psum.tile([P, HALF], F32, name="own_ps%d" % i)
+            product(own_ps[:], w3_q, half(picked_words, i), picked_scales[SCALE_START:, i * HALF : (i + 1) * HALF])
+            nc.scalar.copy(half(own, i), own_ps[:])
+
+        li = work.tile([P, S], F32, name="li")
+        for i, signs in enumerate((sn_first[:], cu_win[:, V:])):
+            nc.vector.tensor_tensor(half(li, i), y[:].indirect(half_list(inc_t, i)), signs, MULT)
+        term_a = work.tile([P, V], F32, name="term_a")
+        term_b = work.tile([P, V], F32, name="term_b", tag="sn_first")
         for i in range(2):
             pairs = half(li, i)
-            nc.vector.tensor_tensor(dv_win[:, i * P : (i + 1) * P], pairs[:, 0::2], pairs[:, 1::2], ADD)
-        nc.vector.tensor_tensor(term_b[:, :P], h[:].indirect(entries(trj_t, 0, P)), sb_t[:, :P], MULT)
-        nc.vector.tensor_tensor(term_a[:], curl_a[:], dv_win[:, V:], MULT)
-        nc.vector.tensor_tensor(term_b[:, P:], curl_b[:], sb_t[:, P:], MULT)
-        for i in range(2):
-            nc.scalar.activation(at_tail[i][:], dv_win[:].indirect(half_list(tail_t, i)), COPY)
-        for i in range(2):
             cols = slice(i * P, (i + 1) * P)
-            nc.vector.tensor_tensor(cu_win[:, cols], term_a[:, cols], term_b[:, cols], ADD)
+            nc.vector.tensor_tensor(dv_win[:, cols], pairs[:, 0::2], pairs[:, 1::2], ADD)
+            nc.vector.tensor_tensor(term_b[:, cols], h[:].indirect(entries(trj_t, cols.start, cols.stop)), sb_t[:, cols], MULT)
+        nc.vector.tensor_tensor(term_a[:], curl_a[:], dv_win[:, V:], MULT)
+
+        at_tail = work.tile([P, S], F32, name="at_tail")
+        at_face = work.tile([P, HALF], F32, name="at_face")
+        own_head = work.tile([P, S], F32, name="own_head")
+        own_down = work.tile([P, S], F32, name="own_down")
+        up = work.tile([P, S], F32, name="up")
+        result = work.tile([P, S], F32, name="result")
+        for i in range(2):
+            nc.scalar.activation(half(at_tail, i), dv_win[:].indirect(half_list(tail_t, i)), COPY)
+        nc.vector.tensor_tensor(half(own_head, 0), dv_win[:].indirect(half_list(head_t, 0)), half(own, 0), ADD)
+        nc.vector.tensor_tensor(cu_win[:, :V], term_a[:], term_b[:], ADD)
+        nc.vector.tensor_tensor(half(own_head, 1), dv_win[:].indirect(half_list(head_t, 1)), half(own, 1), ADD)
         nc.scalar.activation(at_face[:], cu_win[:].indirect(half_list(face_t, 1)), COPY)
         nc.vector.tensor_tensor(half(up, 0), cu_win[:].indirect(half_list(face_t, 0)), half(sf_t, 0), MULT)
-        nc.vector.tensor_tensor(half(down, 0), dv_win[:].indirect(half_list(head_t, 0)), at_tail[0][:], SUB)
-        at_head = work.tile([P, HALF], F32, name="at_head", tag="at_tail0")
-        for lo, hi in Y_PIECES[1:]:
-            nc.scalar.activation(at_head[:, lo - HALF : hi - HALF], dv_win[:].indirect(entries(head_t, lo, hi)), COPY)
-        nc.vector.tensor_tensor(half(down, 1), half(own_ps, 1), at_tail[1][:], SUB)
-        nc.vector.tensor_tensor(half(rest, 0), half(own_ps, 0), half(down, 0), ADD)
+        for i in range(2):
+            nc.vector.tensor_tensor(half(own_down, i), half(own_head, i), half(at_tail, i), SUB)
         nc.vector.tensor_tensor(half(up, 1), at_face[:], half(sf_t, 1), MULT)
-        nc.vector.tensor_tensor(half(result, 0), half(rest, 0), half(up, 0), ADD)
-        nc.sync.dma_start(half(out, 0), half(result, 0))
-        for lo, hi in Y_PIECES[1:]:
-            nc.vector.tensor_tensor(rest[:, lo:hi], down[:, lo:hi], up[:, lo:hi], ADD)
-        for lo, hi in Y_PIECES[1:]:
-            nc.vector.tensor_tensor(result[:, lo:hi], rest[:, lo:hi], at_head[:, lo - HALF : hi - HALF], ADD)
+        for lo, hi in Y_PIECES:
+            nc.vector.tensor_tensor(result[:, lo:hi], own_down[:, lo:hi], up[:, lo:hi], ADD)
             nc.sync.dma_start(out[:, lo:hi], result[:, lo:hi])

@@ -100,17 +100,18 @@ def tile_picked_yhodge_none_p_kernel(
         xw = work.tile([P, T], U32, name="xw", align_bytes=64)
         nc.sync.dma_start(xw[:].bitcast(I32), x_words[0].rearrange("p n t -> p (n t)").bitcast(I32))
         w2_raw = load_weight("w2_raw", w2)
-        trj_t = load_list("trj_t", trj)
         tri_t = load_list("tri_t", tri)
-        sb_t = load_signs("sb_t", sb)
         w3_raw = load_weight("w3_raw", w3)
+        trj_t = load_list("trj_t", trj)
+        dv_win = work.tile([P, 3 * V], F32, name="dv_win")
+        sa_t, sb_t = dv_win[:, V : 2 * V], dv_win[:, 2 * V :]
+        nc.sync.dma_start(sb_t, sb)
         sn_first = work.tile([P, HALF], F32, name="sn_first")
         nc.sync.dma_start(sn_first[:], half(sn, 0))
         cu_win = work.tile([P, 2 * V], F32, name="cu_win")
         nc.sync.dma_start(cu_win[:, V:], half(sn, 1))
         inc_t = load_list("inc_t", inc)
-        dv_win = work.tile([P, 2 * V], F32, name="dv_win")
-        nc.sync.dma_start(dv_win[:, V:], sa)
+        nc.sync.dma_start(sa_t, sa)
         head_t = load_list("head_t", head)
         sf_t = work.tile([P, S], F32, name="sf_t")
         for i in range(2):
@@ -145,10 +146,10 @@ def tile_picked_yhodge_none_p_kernel(
         curl_a = work.tile([P, V], F32, name="curl_a")
         nc.scalar.activation(curl_a[:], h[:].indirect(tri_t[:]), COPY)
         own = work.tile([P, S], F32, name="own")
+        own_ps = psum.tile([P, S], F32, name="own_ps")
+        product(own_ps[:], w3_q, picked_words[:], picked_scales[SCALE_START:, :])
         for i in range(2):
-            own_ps = psum.tile([P, HALF], F32, name="own_ps%d" % i)
-            product(own_ps[:], w3_q, half(picked_words, i), picked_scales[SCALE_START:, i * HALF : (i + 1) * HALF])
-            nc.scalar.copy(half(own, i), own_ps[:])
+            nc.scalar.copy(half(own, i), half(own_ps, i))
 
         li = work.tile([P, S], F32, name="li")
         for i, signs in enumerate((sn_first[:], cu_win[:, V:])):
@@ -160,7 +161,7 @@ def tile_picked_yhodge_none_p_kernel(
             cols = slice(i * P, (i + 1) * P)
             nc.vector.tensor_tensor(dv_win[:, cols], pairs[:, 0::2], pairs[:, 1::2], ADD)
             nc.vector.tensor_tensor(term_b[:, cols], h[:].indirect(entries(trj_t, cols.start, cols.stop)), sb_t[:, cols], MULT)
-        nc.vector.tensor_tensor(term_a[:], curl_a[:], dv_win[:, V:], MULT)
+        nc.vector.tensor_tensor(term_a[:], curl_a[:], sa_t, MULT)
 
         at_tail = work.tile([P, S], F32, name="at_tail")
         at_face = work.tile([P, HALF], F32, name="at_face")
@@ -168,8 +169,7 @@ def tile_picked_yhodge_none_p_kernel(
         own_down = work.tile([P, S], F32, name="own_down")
         up = work.tile([P, S], F32, name="up")
         result = work.tile([P, S], F32, name="result")
-        for i in range(2):
-            nc.scalar.activation(half(at_tail, i), dv_win[:].indirect(half_list(tail_t, i)), COPY)
+        nc.scalar.activation(at_tail[:], dv_win[:].indirect(tail_t[:]), COPY)
         nc.vector.tensor_tensor(half(own_head, 0), dv_win[:].indirect(half_list(head_t, 0)), half(own, 0), ADD)
         nc.vector.tensor_tensor(cu_win[:, :V], term_a[:], term_b[:], ADD)
         nc.vector.tensor_tensor(half(own_head, 1), dv_win[:].indirect(half_list(head_t, 1)), half(own, 1), ADD)

@@ -1,6 +1,7 @@
 from contextlib import ExitStack
 
 import concourse.mybir as mybir
+from concourse.masks import make_identity
 
 K, T, S, N, V = 512, 2048, 512, 128, 256
 FLOPS = 3 * 2 * K * N * S
@@ -88,6 +89,8 @@ def tile_picked_yhodge_none_p_kernel(
 
         xs = work.tile([P, T], U8, name="xs", align_bytes=64)
         nc.vector.memset(xs[:].bitcast(I32), 0)
+        ident = work.tile([P, P], F32, name="ident")
+        make_identity(nc, ident[:])
 
         w1_raw = load_weight("w1_raw", w1)
         offs_t = load_list("offs_t", offs)
@@ -113,9 +116,10 @@ def tile_picked_yhodge_none_p_kernel(
         inc_t = load_list("inc_t", inc)
         nc.sync.dma_start(sa_t, sa)
         head_t = load_list("head_t", head)
-        sf_t = work.tile([P, S], F32, name="sf_t")
-        for i in range(2):
-            nc.sync.dma_start(half(sf_t, i), half(sf, i))
+        sf_cols = work.tile([P, S // P], F32, name="sf_cols")
+        nc.sync.dma_start(sf_cols[:], sf[0].rearrange("(p c) -> p c", p=P))
+        sf_t = work.tile([P, P], F32, name="sf_t")
+        nc.sync.dma_start(sf_t[:], sf[:, :P])
         tail_t = load_list("tail_t", tail)
         face_t = load_list("face_t", face)
 
@@ -144,40 +148,61 @@ def tile_picked_yhodge_none_p_kernel(
 
         w3_q = quantise("w3", w3_bf, "w2_bf")
         curl_a = work.tile([P, V], F32, name="curl_a")
+        curl_b = work.tile([P, P], F32, name="curl_b")
         nc.scalar.activation(curl_a[:], h[:].indirect(tri_t[:]), COPY)
-        own = work.tile([P, S], F32, name="own")
+        nc.scalar.activation(curl_b[:], h[:].indirect(entries(trj_t, P, V)), COPY)
+        own = work.tile([P, HALF], F32, name="own", tag="w2_raw")
         own_ps = psum.tile([P, S], F32, name="own_ps")
         product(own_ps[:], w3_q, picked_words[:], picked_scales[SCALE_START:, :])
-        for i in range(2):
-            nc.scalar.copy(half(own, i), half(own_ps, i))
+        nc.scalar.copy(own[:], half(own_ps, 0))
+
+        sf_ps = psum.tile([P, S // P, P], F32, name="sf_ps")
+        for c in range(S // P):
+            nc.tensor.transpose(sf_ps[:, c, :], sf_cols[:, c : c + 1].to_broadcast([P, P]), ident[:])
+        sf_row = sf_ps[:].rearrange("p c n -> p n c")
 
         li = work.tile([P, S], F32, name="li")
         for i, signs in enumerate((sn_first[:], cu_win[:, V:])):
             nc.vector.tensor_tensor(half(li, i), y[:].indirect(half_list(inc_t, i)), signs, MULT)
         term_a = work.tile([P, V], F32, name="term_a")
         term_b = work.tile([P, V], F32, name="term_b", tag="sn_first")
-        for i in range(2):
-            pairs = half(li, i)
-            cols = slice(i * P, (i + 1) * P)
-            nc.vector.tensor_tensor(dv_win[:, cols], pairs[:, 0::2], pairs[:, 1::2], ADD)
-            nc.vector.tensor_tensor(term_b[:, cols], h[:].indirect(entries(trj_t, cols.start, cols.stop)), sb_t[:, cols], MULT)
-        nc.vector.tensor_tensor(term_a[:], curl_a[:], sa_t, MULT)
 
-        at_tail = work.tile([P, S], F32, name="at_tail")
-        at_face = work.tile([P, HALF], F32, name="at_face")
-        own_head = work.tile([P, S], F32, name="own_head")
-        own_down = work.tile([P, S], F32, name="own_down")
+        def pair_sum(i):
+            pairs = half(li, i)
+            nc.vector.tensor_tensor(dv_win[:, i * P : (i + 1) * P], pairs[:, 0::2], pairs[:, 1::2], ADD)
+
+        pair_sum(0)
+        nc.vector.tensor_tensor(term_b[:, :P], h[:].indirect(entries(trj_t, 0, P)), sb_t[:, :P], MULT)
+        pair_sum(1)
+        nc.vector.tensor_tensor(term_a[:], curl_a[:], sa_t, MULT)
+        nc.vector.tensor_tensor(term_b[:, P:], curl_b[:], sb_t[:, P:], MULT)
+
+        at_tail = [work.tile([P, HALF], F32, name="at_tail%d" % i) for i in range(2)]
+        at_face = work.tile([P, S], F32, name="at_face")
+        part = work.tile([P, S], F32, name="part")
         up = work.tile([P, S], F32, name="up")
         result = work.tile([P, S], F32, name="result")
-        nc.scalar.activation(at_tail[:], dv_win[:].indirect(tail_t[:]), COPY)
-        nc.vector.tensor_tensor(half(own_head, 0), dv_win[:].indirect(half_list(head_t, 0)), half(own, 0), ADD)
+        for i in (1, 0):
+            nc.scalar.activation(at_tail[i][:], dv_win[:].indirect(half_list(tail_t, i)), COPY)
+        nc.vector.tensor_tensor(half(part, 0), dv_win[:].indirect(half_list(head_t, 0)), own[:], ADD)
         nc.vector.tensor_tensor(cu_win[:, :V], term_a[:], term_b[:], ADD)
-        nc.vector.tensor_tensor(half(own_head, 1), dv_win[:].indirect(half_list(head_t, 1)), half(own, 1), ADD)
-        nc.scalar.activation(at_face[:], cu_win[:].indirect(half_list(face_t, 1)), COPY)
-        nc.vector.tensor_tensor(half(up, 0), cu_win[:].indirect(half_list(face_t, 0)), half(sf_t, 0), MULT)
-        for i in range(2):
-            nc.vector.tensor_tensor(half(own_down, i), half(own_head, i), half(at_tail, i), SUB)
-        nc.vector.tensor_tensor(half(up, 1), at_face[:], half(sf_t, 1), MULT)
-        for lo, hi in Y_PIECES:
-            nc.vector.tensor_tensor(result[:, lo:hi], own_down[:, lo:hi], up[:, lo:hi], ADD)
+        nc.vector.tensor_tensor(half(part, 1), dv_win[:].indirect(half_list(head_t, 1)), at_tail[1][:], SUB)
+        for lo, hi in ((HALF, S), (P, HALF)):
+            nc.scalar.activation(at_face[:, lo:hi], cu_win[:].indirect(entries(face_t, lo, hi)), COPY)
+        first = work.tile([P, HALF], F32, name="first", tag="at_tail1")
+        nc.gpsimd.tensor_tensor(first[:], half(part, 0), at_tail[0][:], SUB)
+        nc.vector.tensor_tensor(up[:, :P], cu_win[:].indirect(entries(face_t, 0, P)), sf_t[:, :P], MULT)
+        second = work.tile([P, HALF], F32, name="second")
+        nc.vector.tensor_tensor(second[:], half(own_ps, 1), half(part, 1), ADD)
+        for lo, hi in ((HALF, S), (P, HALF)):
+            c = S // P
+            nc.vector.tensor_tensor(
+                up[:, lo:hi].rearrange("p (n c) -> p n c", c=c),
+                sf_row[:, lo // c : hi // c, :],
+                at_face[:, lo:hi].rearrange("p (n c) -> p n c", c=c),
+                MULT,
+            )
+        for lo, hi in ((HALF, S), (0, P), (P, HALF)):
+            own_down = first[:, lo:hi] if lo < HALF else second[:]
+            nc.vector.tensor_tensor(result[:, lo:hi], own_down, up[:, lo:hi], ADD)
             nc.sync.dma_start(out[:, lo:hi], result[:, lo:hi])

@@ -26,6 +26,7 @@ SCALE_ROWS = 4
 SCALE_START = 12
 LIST_COL = 16
 HALF = S // 2
+SPREAD = S // P - 1
 Y_PIECES = ((0, HALF), (HALF, HALF + P), (HALF + P, S))
 
 
@@ -116,8 +117,9 @@ def tile_picked_yhodge_none_p_kernel(
         inc_t = load_list("inc_t", inc)
         nc.sync.dma_start(sa_t, sa)
         head_t = load_list("head_t", head)
-        sf_cols = work.tile([P, S // P], F32, name="sf_cols")
-        nc.sync.dma_start(sf_cols[:], sf[0].rearrange("(p c) -> p c", p=P))
+        sf_cols = work.tile([P, SPREAD], F32, name="sf_cols")
+        with nc.allow_non_contiguous_dma(reason="one sign a partition and square"):
+            nc.sync.dma_start(sf_cols[:], sf[0, P:].rearrange("(c p) -> p c", p=P))
         sf_t = work.tile([P, P], F32, name="sf_t")
         nc.sync.dma_start(sf_t[:], sf[:, :P])
         tail_t = load_list("tail_t", tail)
@@ -156,10 +158,9 @@ def tile_picked_yhodge_none_p_kernel(
         product(own_ps[:], w3_q, picked_words[:], picked_scales[SCALE_START:, :])
         nc.scalar.copy(own[:], half(own_ps, 0))
 
-        sf_ps = psum.tile([P, S // P, P], F32, name="sf_ps")
-        for c in range(S // P):
-            nc.tensor.transpose(sf_ps[:, c, :], sf_cols[:, c : c + 1].to_broadcast([P, P]), ident[:])
-        sf_row = sf_ps[:].rearrange("p c n -> p n c")
+        sf_ps = psum.tile([P, SPREAD * P], F32, name="sf_ps")
+        for c in range(SPREAD):
+            nc.tensor.transpose(sf_ps[:, c * P : (c + 1) * P], sf_cols[:, c : c + 1].to_broadcast([P, P]), ident[:])
 
         li = work.tile([P, S], F32, name="li")
         for i, signs in enumerate((sn_first[:], cu_win[:, V:])):
@@ -193,15 +194,9 @@ def tile_picked_yhodge_none_p_kernel(
         nc.gpsimd.tensor_tensor(first[:], half(part, 0), at_tail[0][:], SUB)
         nc.vector.tensor_tensor(up[:, :P], cu_win[:].indirect(entries(face_t, 0, P)), sf_t[:, :P], MULT)
         second = work.tile([P, HALF], F32, name="second")
-        nc.vector.tensor_tensor(second[:], half(own_ps, 1), half(part, 1), ADD)
+        nc.vector.tensor_tensor(second[:], half(part, 1), half(own_ps, 1), ADD)
         for lo, hi in ((HALF, S), (P, HALF)):
-            c = S // P
-            nc.vector.tensor_tensor(
-                up[:, lo:hi].rearrange("p (n c) -> p n c", c=c),
-                sf_row[:, lo // c : hi // c, :],
-                at_face[:, lo:hi].rearrange("p (n c) -> p n c", c=c),
-                MULT,
-            )
+            nc.vector.tensor_tensor(up[:, lo:hi], at_face[:, lo:hi], sf_ps[:, lo - P : hi - P], MULT)
         for lo, hi in ((HALF, S), (0, P), (P, HALF)):
             own_down = first[:, lo:hi] if lo < HALF else second[:]
             nc.vector.tensor_tensor(result[:, lo:hi], own_down, up[:, lo:hi], ADD)

@@ -150,9 +150,7 @@ def tile_picked_yhodge_none_p_kernel(
 
         w3_q = quantise("w3", w3_bf, "w2_bf")
         curl_a = work.tile([P, V], F32, name="curl_a")
-        curl_b = work.tile([P, P], F32, name="curl_b")
         nc.scalar.activation(curl_a[:], h[:].indirect(tri_t[:]), COPY)
-        nc.scalar.activation(curl_b[:], h[:].indirect(entries(trj_t, P, V)), COPY)
         own = work.tile([P, HALF], F32, name="own", tag="w2_raw")
         own_ps = psum.tile([P, S], F32, name="own_ps")
         product(own_ps[:], w3_q, picked_words[:], picked_scales[SCALE_START:, :])
@@ -168,15 +166,12 @@ def tile_picked_yhodge_none_p_kernel(
         term_a = work.tile([P, V], F32, name="term_a")
         term_b = work.tile([P, V], F32, name="term_b", tag="sn_first")
 
-        def pair_sum(i):
+        for i in range(2):
             pairs = half(li, i)
-            nc.vector.tensor_tensor(dv_win[:, i * P : (i + 1) * P], pairs[:, 0::2], pairs[:, 1::2], ADD)
-
-        pair_sum(0)
-        nc.vector.tensor_tensor(term_b[:, :P], h[:].indirect(entries(trj_t, 0, P)), sb_t[:, :P], MULT)
-        pair_sum(1)
+            cols = slice(i * P, (i + 1) * P)
+            nc.vector.tensor_tensor(dv_win[:, cols], pairs[:, 0::2], pairs[:, 1::2], ADD)
+            nc.vector.tensor_tensor(term_b[:, cols], h[:].indirect(entries(trj_t, cols.start, cols.stop)), sb_t[:, cols], MULT)
         nc.vector.tensor_tensor(term_a[:], curl_a[:], sa_t, MULT)
-        nc.vector.tensor_tensor(term_b[:, P:], curl_b[:], sb_t[:, P:], MULT)
 
         at_tail = [work.tile([P, HALF], F32, name="at_tail%d" % i) for i in range(2)]
         at_face = work.tile([P, S], F32, name="at_face")

@@ -27,6 +27,7 @@ SCALE_START = 12
 LIST_COL = 16
 HALF = S // 2
 SPREAD = S // P - 1
+ROUND_SPLIT = 3 * N // 4
 Y_PIECES = ((0, HALF), (HALF, HALF + P), (HALF + P, S))
 
 
@@ -130,7 +131,9 @@ def tile_picked_yhodge_none_p_kernel(
         nc.vector.tensor_copy(picked_scales[:], xs[:].indirect(offs_t[:]))
         w1_q = quantise("w1", w1_bf, "w1_codes")
 
-        w2_bf = round_weight("w2_bf", w2_raw, nc.scalar.copy)
+        w2_bf = work.tile([P, N, PACK], BF16, name="w2_bf", align_bytes=64)
+        for copy, cols in ((nc.scalar.copy, slice(0, ROUND_SPLIT)), (nc.gpsimd.tensor_copy, slice(ROUND_SPLIT, N))):
+            copy(w2_bf[:, cols, :], w2_raw[:, :, cols].rearrange("p j n -> p n j"))
         picked_words = work.tile([P, S], U32, name="picked_words", align_bytes=64)
         y = work.tile([P, S], F32, name="y", tag="w2_raw")
         for lo, hi in Y_PIECES:

@@ -188,14 +188,15 @@ def tile_picked_yhodge_none_p_kernel(
         nc.vector.tensor_tensor(half(part, 1), dv_win[:].indirect(half_list(head_t, 1)), at_tail[1][:], SUB)
         for lo, hi in ((HALF, S), (P, HALF)):
             nc.scalar.activation(at_face[:, lo:hi], cu_win[:].indirect(entries(face_t, lo, hi)), COPY)
-        first = work.tile([P, HALF], F32, name="first", tag="at_tail1")
-        nc.gpsimd.tensor_tensor(first[:], half(part, 0), at_tail[0][:], SUB)
+        first = [work.tile([P, P], F32, name="first0"), work.tile([P, P], F32, name="first1", tag="at_tail1")]
+        nc.vector.tensor_tensor(first[0][:], part[:, :P], at_tail[0][:, :P], SUB)
+        nc.gpsimd.tensor_tensor(first[1][:], part[:, P:HALF], at_tail[0][:, P:], SUB)
         nc.vector.tensor_tensor(up[:, :P], cu_win[:].indirect(entries(face_t, 0, P)), sf_t[:, :P], MULT)
         second = work.tile([P, HALF], F32, name="second")
         nc.vector.tensor_tensor(second[:], half(part, 1), half(own_ps, 1), ADD)
-        for lo, hi in ((HALF, S), (P, HALF)):
-            nc.vector.tensor_tensor(up[:, lo:hi], at_face[:, lo:hi], sf_ps[:, lo - P : hi - P], MULT)
-        for lo, hi in ((HALF, S), (0, P), (P, HALF)):
-            own_down = first[:, lo:hi] if lo < HALF else second[:]
+        nc.vector.tensor_tensor(half(up, 1), half(at_face, 1), sf_ps[:, P:], MULT)
+        nc.vector.tensor_tensor(up[:, P:HALF], at_face[:, P:HALF], sf_ps[:, :P], MULT)
+        for lo, hi in ((0, P), (HALF, S), (P, HALF)):
+            own_down = first[lo // P][:] if lo < HALF else second[:]
             nc.vector.tensor_tensor(result[:, lo:hi], own_down, up[:, lo:hi], ADD)
             nc.sync.dma_start(out[:, lo:hi], result[:, lo:hi])

@@ -28,6 +28,7 @@ LIST_COL = 16
 HALF = S // 2
 SPREAD = S // P - 1
 ROUND_SPLIT = 3 * N // 4
+LAST_END = HALF + P // 2
 Y_PIECES = ((0, HALF), (HALF, HALF + P), (HALF + P, S))
 
 
@@ -118,9 +119,10 @@ def tile_picked_yhodge_none_p_kernel(
         inc_t = load_list("inc_t", inc)
         nc.sync.dma_start(sa_t, sa)
         head_t = load_list("head_t", head)
-        sf_cols = work.tile([P, SPREAD], F32, name="sf_cols")
+        part = work.tile([P, S], F32, name="part")
+        sf_cols = part[:, P : P + SPREAD]
         with nc.allow_non_contiguous_dma(reason="one sign a partition and square"):
-            nc.sync.dma_start(sf_cols[:], sf[0, P:].rearrange("(c p) -> p c", p=P))
+            nc.sync.dma_start(sf_cols, sf[0, P:].rearrange("(c p) -> p c", p=P))
         sf_t = work.tile([P, P], F32, name="sf_t")
         nc.sync.dma_start(sf_t[:], sf[:, :P])
         tail_t = load_list("tail_t", tail)
@@ -176,27 +178,31 @@ def tile_picked_yhodge_none_p_kernel(
             nc.vector.tensor_tensor(term_b[:, cols], h[:].indirect(entries(trj_t, cols.start, cols.stop)), sb_t[:, cols], MULT)
         nc.vector.tensor_tensor(term_a[:], curl_a[:], sa_t, MULT)
 
-        at_tail = [work.tile([P, HALF], F32, name="at_tail%d" % i) for i in range(2)]
+        own_down = work.tile([P, S], F32, name="own_down")
+        tail_second = own_down[:, P : P + HALF]
+        tail_b = work.tile([P, P], F32, name="tail_b")
         at_face = work.tile([P, S], F32, name="at_face")
-        part = work.tile([P, S], F32, name="part")
         up = work.tile([P, S], F32, name="up")
         result = work.tile([P, S], F32, name="result")
-        for i in (1, 0):
-            nc.scalar.activation(at_tail[i][:], dv_win[:].indirect(half_list(tail_t, i)), COPY)
-        nc.vector.tensor_tensor(half(part, 0), dv_win[:].indirect(half_list(head_t, 0)), own[:], ADD)
+        nc.scalar.activation(tail_second, dv_win[:].indirect(half_list(tail_t, 1)), COPY)
+        nc.scalar.activation(tail_b[:], dv_win[:].indirect(entries(tail_t, P, HALF)), COPY)
+        nc.vector.tensor_tensor(part[:, :P], dv_win[:].indirect(entries(head_t, 0, P)), own[:, :P], ADD)
         nc.vector.tensor_tensor(cu_win[:, :V], term_a[:], term_b[:], ADD)
-        nc.vector.tensor_tensor(half(part, 1), dv_win[:].indirect(half_list(head_t, 1)), at_tail[1][:], SUB)
+        nc.vector.tensor_tensor(part[:, P:HALF], dv_win[:].indirect(entries(head_t, P, HALF)), own[:, P:], ADD)
+        nc.vector.tensor_tensor(half(part, 1), dv_win[:].indirect(half_list(head_t, 1)), tail_second, SUB)
         for lo, hi in ((HALF, S), (P, HALF)):
             nc.scalar.activation(at_face[:, lo:hi], cu_win[:].indirect(entries(face_t, lo, hi)), COPY)
-        first = [work.tile([P, P], F32, name="first0"), work.tile([P, P], F32, name="first1", tag="at_tail1")]
-        nc.vector.tensor_tensor(first[0][:], part[:, :P], at_tail[0][:, :P], SUB)
-        nc.gpsimd.tensor_tensor(first[1][:], part[:, P:HALF], at_tail[0][:, P:], SUB)
-        nc.vector.tensor_tensor(up[:, :P], cu_win[:].indirect(entries(face_t, 0, P)), sf_t[:, :P], MULT)
-        second = work.tile([P, HALF], F32, name="second")
-        nc.vector.tensor_tensor(second[:], half(part, 1), half(own_ps, 1), ADD)
+        nc.vector.tensor_tensor(up[:, :P], cu_win[:].indirect(entries(face_t, 0, P)), sf_t[:], MULT)
+        nc.scalar.activation(sf_t[:], dv_win[:].indirect(entries(tail_t, 0, P)), COPY)
+        nc.gpsimd.tensor_tensor(own_down[:, P:HALF], part[:, P:HALF], tail_b[:], SUB)
+        nc.vector.tensor_tensor(half(own_down, 1), half(part, 1), half(own_ps, 1), ADD)
         nc.vector.tensor_tensor(half(up, 1), half(at_face, 1), sf_ps[:, P:], MULT)
+        own_head_up = part[:, HALF : HALF + P]
+        nc.vector.tensor_tensor(own_head_up, part[:, :P], up[:, :P], ADD)
         nc.vector.tensor_tensor(up[:, P:HALF], at_face[:, P:HALF], sf_ps[:, :P], MULT)
-        for lo, hi in ((0, P), (HALF, S), (P, HALF)):
-            own_down = first[lo // P][:] if lo < HALF else second[:]
-            nc.vector.tensor_tensor(result[:, lo:hi], own_down, up[:, lo:hi], ADD)
+        for lo, hi in ((LAST_END, S), (0, P), (P, LAST_END)):
+            if lo == 0:
+                nc.vector.tensor_tensor(result[:, :P], own_head_up, sf_t[:], SUB)
+            else:
+                nc.vector.tensor_tensor(result[:, lo:hi], own_down[:, lo:hi], up[:, lo:hi], ADD)
             nc.sync.dma_start(out[:, lo:hi], result[:, lo:hi])

@@ -29,6 +29,8 @@ HALF = S // 2
 SPREAD = S // P - 1
 ROUND_SPLIT = 3 * N // 4
 LAST_END = HALF + P // 2
+REGION = 32 * 1024
+SLOT = 4 * S
 Y_PIECES = ((0, HALF), (HALF, HALF + P), (HALF + P, S))
 
 
@@ -39,6 +41,7 @@ def tile_picked_yhodge_none_p_kernel(
     with ExitStack() as ctx:
         lists = ctx.enter_context(tc.tile_pool(name="lists", bufs=1))
         work = ctx.enter_context(tc.tile_pool(name="work", bufs=1))
+        apart = ctx.enter_context(tc.tile_pool(name="apart", bufs=1))
         psum = ctx.enter_context(tc.psum_pool(name="psum", bufs=1))
 
         def load_list(name, src):
@@ -51,8 +54,12 @@ def tile_picked_yhodge_none_p_kernel(
             nc.sync.dma_start(tile[:], src)
             return tile
 
-        def load_weight(name, src):
-            tile = work.tile([P, PACK, N], F32, name=name)
+        def far_tile(name, shape, region, slot=0):
+            return apart.tile(shape, F32, name=name, offset=(region + 1) * REGION + slot * SLOT)
+
+        def load_weight(name, src, tile=None):
+            if tile is None:
+                tile = work.tile([P, PACK, N], F32, name=name)
             nc.sync.dma_start(tile[:], src.rearrange("(p j) n -> p j n", j=PACK))
             return tile
 
@@ -105,16 +112,16 @@ def tile_picked_yhodge_none_p_kernel(
             )
         xw = work.tile([P, T], U32, name="xw", align_bytes=64)
         nc.sync.dma_start(xw[:].bitcast(I32), x_words[0].rearrange("p n t -> p (n t)").bitcast(I32))
-        w2_raw = load_weight("w2_raw", w2)
+        w2_raw = load_weight("w2_raw", w2, far_tile("w2_raw", [P, PACK, N], 0))
         tri_t = load_list("tri_t", tri)
         w3_raw = load_weight("w3_raw", w3)
         trj_t = load_list("trj_t", trj)
-        dv_win = work.tile([P, 3 * V], F32, name="dv_win")
+        dv_win = far_tile("dv_win", [P, 3 * V], 2)
         sa_t, sb_t = dv_win[:, V : 2 * V], dv_win[:, 2 * V :]
         nc.sync.dma_start(sb_t, sb)
         sn_first = work.tile([P, HALF], F32, name="sn_first")
         nc.sync.dma_start(sn_first[:], half(sn, 0))
-        cu_win = work.tile([P, 2 * V], F32, name="cu_win")
+        cu_win = far_tile("cu_win", [P, 2 * V], 3)
         nc.sync.dma_start(cu_win[:, V:], half(sn, 1))
         inc_t = load_list("inc_t", inc)
         nc.sync.dma_start(sa_t, sa)
@@ -123,7 +130,7 @@ def tile_picked_yhodge_none_p_kernel(
         sf_cols = part[:, P : P + SPREAD]
         with nc.allow_non_contiguous_dma(reason="one sign a partition and square"):
             nc.sync.dma_start(sf_cols, sf[0, P:].rearrange("(c p) -> p c", p=P))
-        sf_t = work.tile([P, P], F32, name="sf_t")
+        sf_t = far_tile("sf_t", [P, P], 4, 4)
         nc.sync.dma_start(sf_t[:], sf[:, :P])
         tail_t = load_list("tail_t", tail)
         face_t = load_list("face_t", face)
@@ -137,7 +144,7 @@ def tile_picked_yhodge_none_p_kernel(
         for copy, cols in ((nc.scalar.copy, slice(0, ROUND_SPLIT)), (nc.gpsimd.tensor_copy, slice(ROUND_SPLIT, N))):
             copy(w2_bf[:, cols, :], w2_raw[:, :, cols].rearrange("p j n -> p n j"))
         picked_words = work.tile([P, S], U32, name="picked_words", align_bytes=64)
-        y = work.tile([P, S], F32, name="y", tag="w2_raw")
+        y = far_tile("y", [P, S], 0)
         for lo, hi in Y_PIECES:
             nc.vector.tensor_copy(picked_words[:, lo:hi], xw[:].indirect(entries(offs_t, lo, hi)))
         for piece, (lo, hi) in enumerate(Y_PIECES):
@@ -147,16 +154,16 @@ def tile_picked_yhodge_none_p_kernel(
 
         w2_q = quantise("w2", w2_bf, "w2_codes")
         w3_bf = round_weight("w3_bf", w3_raw, nc.vector.tensor_copy)
-        h = work.tile([P, S], F32, name="h")
+        h = far_tile("h", [P, S], 1)
         for piece, (lo, hi) in enumerate(Y_PIECES):
             h_ps = psum.tile([P, hi - lo], F32, name="h_ps%d" % piece)
             product(h_ps[:], w2_q, picked_words[:, lo:hi], picked_scales[SCALE_START:, lo:hi])
             nc.scalar.copy(h[:, lo:hi], h_ps[:])
 
         w3_q = quantise("w3", w3_bf, "w2_bf")
-        curl_a = work.tile([P, V], F32, name="curl_a")
+        curl_a = far_tile("curl_a", [P, V], 4)
         nc.scalar.activation(curl_a[:], h[:].indirect(tri_t[:]), COPY)
-        own = work.tile([P, HALF], F32, name="own", tag="w2_raw")
+        own = far_tile("own", [P, HALF], 0)
         own_ps = psum.tile([P, S], F32, name="own_ps")
         product(own_ps[:], w3_q, picked_words[:], picked_scales[SCALE_START:, :])
         nc.scalar.copy(own[:], half(own_ps, 0))
@@ -178,10 +185,10 @@ def tile_picked_yhodge_none_p_kernel(
             nc.vector.tensor_tensor(term_b[:, cols], h[:].indirect(entries(trj_t, cols.start, cols.stop)), sb_t[:, cols], MULT)
         nc.vector.tensor_tensor(term_a[:], curl_a[:], sa_t, MULT)
 
-        own_down = work.tile([P, S], F32, name="own_down")
+        own_down = far_tile("own_down", [P, S], 4, 1)
         tail_second = own_down[:, P : P + HALF]
-        tail_b = work.tile([P, P], F32, name="tail_b")
-        at_face = work.tile([P, S], F32, name="at_face")
+        tail_b = far_tile("tail_b", [P, P], 4, 2)
+        at_face = far_tile("at_face", [P, S], 4, 3)
         up = work.tile([P, S], F32, name="up")
         result = work.tile([P, S], F32, name="result")
         nc.scalar.activation(tail_second, dv_win[:].indirect(half_list(tail_t, 1)), COPY)

@@ -113,8 +113,8 @@ def tile_picked_yhodge_none_p_kernel(
         xw = work.tile([P, T], U32, name="xw", align_bytes=64)
         nc.sync.dma_start(xw[:].bitcast(I32), x_words[0].rearrange("p n t -> p (n t)").bitcast(I32))
         w2_raw = load_weight("w2_raw", w2, far_tile("w2_raw", [P, PACK, N], 0))
-        tri_t = load_list("tri_t", tri)
         w3_raw = load_weight("w3_raw", w3)
+        tri_t = load_list("tri_t", tri)
         trj_t = load_list("trj_t", trj)
         dv_win = far_tile("dv_win", [P, 3 * V], 2)
         sa_t, sb_t = dv_win[:, V : 2 * V], dv_win[:, 2 * V :]
@@ -152,8 +152,8 @@ def tile_picked_yhodge_none_p_kernel(
             product(y_ps[:], w1_q, picked_words[:, lo:hi], picked_scales[SCALE_START:, lo:hi])
             nc.scalar.copy(y[:, lo:hi], y_ps[:])
 
-        w2_q = quantise("w2", w2_bf, "w2_codes")
         w3_bf = round_weight("w3_bf", w3_raw, nc.vector.tensor_copy)
+        w2_q = quantise("w2", w2_bf, "w2_codes")
         h = far_tile("h", [P, S], 1)
         for piece, (lo, hi) in enumerate(Y_PIECES):
             h_ps = psum.tile([P, hi - lo], F32, name="h_ps%d" % piece)
@@ -205,9 +205,9 @@ def tile_picked_yhodge_none_p_kernel(
         nc.vector.tensor_tensor(half(own_down, 1), half(part, 1), half(own_ps, 1), ADD)
         nc.vector.tensor_tensor(half(up, 1), half(at_face, 1), sf_ps[:, P:], MULT)
         own_head_up = part[:, HALF : HALF + P]
-        nc.vector.tensor_tensor(own_head_up, part[:, :P], up[:, :P], ADD)
         nc.vector.tensor_tensor(up[:, P:HALF], at_face[:, P:HALF], sf_ps[:, :P], MULT)
-        for lo, hi in ((LAST_END, S), (0, P), (P, LAST_END)):
+        nc.vector.tensor_tensor(own_head_up, part[:, :P], up[:, :P], ADD)
+        for lo, hi in ((LAST_END, S), (P, LAST_END), (0, P)):
             if lo == 0:
                 nc.vector.tensor_tensor(result[:, :P], own_head_up, sf_t[:], SUB)
             else:

@@ -31,6 +31,7 @@ ROUND_SPLIT = 3 * N // 4
 LAST_END = HALF + P // 2
 REGION = 32 * 1024
 SLOT = 4 * S
+POOL_END = P + 3 * P // 2
 Y_PIECES = ((0, HALF), (HALF, HALF + P), (HALF + P, S))
 
 
@@ -163,10 +164,10 @@ def tile_picked_yhodge_none_p_kernel(
         w3_q = quantise("w3", w3_bf, "w2_bf")
         curl_a = far_tile("curl_a", [P, V], 4)
         nc.scalar.activation(curl_a[:], h[:].indirect(tri_t[:]), COPY)
-        own = far_tile("own", [P, HALF], 0)
+        own = far_tile("own", [P, POOL_END], 0)
         own_ps = psum.tile([P, S], F32, name="own_ps")
         product(own_ps[:], w3_q, picked_words[:], picked_scales[SCALE_START:, :])
-        nc.scalar.copy(own[:], half(own_ps, 0))
+        nc.scalar.copy(own[:], own_ps[:, :POOL_END])
 
         sf_ps = psum.tile([P, SPREAD * P], F32, name="sf_ps")
         for c in range(SPREAD):
@@ -186,25 +187,25 @@ def tile_picked_yhodge_none_p_kernel(
         nc.vector.tensor_tensor(term_a[:], curl_a[:], sa_t, MULT)
 
         own_down = far_tile("own_down", [P, S], 4, 1)
-        tail_second = own_down[:, P : P + HALF]
-        tail_b = far_tile("tail_b", [P, P], 4, 2)
+        tail_second = own_down[:, P : P + S - POOL_END]
+        tail_b = far_tile("tail_b", [P, POOL_END - P], 4, 2)
         at_face = far_tile("at_face", [P, S], 4, 3)
         up = work.tile([P, S], F32, name="up")
         result = work.tile([P, S], F32, name="result")
-        nc.scalar.activation(tail_second, dv_win[:].indirect(half_list(tail_t, 1)), COPY)
-        nc.scalar.activation(tail_b[:], dv_win[:].indirect(entries(tail_t, P, HALF)), COPY)
+        nc.scalar.activation(tail_second, dv_win[:].indirect(entries(tail_t, POOL_END, S)), COPY)
+        nc.scalar.activation(tail_b[:], dv_win[:].indirect(entries(tail_t, P, POOL_END)), COPY)
         nc.vector.tensor_tensor(part[:, :P], dv_win[:].indirect(entries(head_t, 0, P)), own[:, :P], ADD)
         nc.vector.tensor_tensor(cu_win[:, :V], term_a[:], term_b[:], ADD)
-        nc.vector.tensor_tensor(part[:, P:HALF], dv_win[:].indirect(entries(head_t, P, HALF)), own[:, P:], ADD)
-        nc.vector.tensor_tensor(half(part, 1), dv_win[:].indirect(half_list(head_t, 1)), tail_second, SUB)
+        nc.vector.tensor_tensor(part[:, P:POOL_END], dv_win[:].indirect(entries(head_t, P, POOL_END)), own[:, P:], ADD)
+        nc.vector.tensor_tensor(part[:, POOL_END:], dv_win[:].indirect(entries(head_t, POOL_END, S)), tail_second, SUB)
         for lo, hi in ((HALF, S), (P, HALF)):
             nc.scalar.activation(at_face[:, lo:hi], cu_win[:].indirect(entries(face_t, lo, hi)), COPY)
         nc.vector.tensor_tensor(up[:, :P], cu_win[:].indirect(entries(face_t, 0, P)), sf_t[:], MULT)
         nc.scalar.activation(sf_t[:], dv_win[:].indirect(entries(tail_t, 0, P)), COPY)
-        nc.gpsimd.tensor_tensor(own_down[:, P:HALF], part[:, P:HALF], tail_b[:], SUB)
-        nc.vector.tensor_tensor(half(own_down, 1), half(part, 1), half(own_ps, 1), ADD)
+        nc.gpsimd.tensor_tensor(own_down[:, P:POOL_END], part[:, P:POOL_END], tail_b[:], SUB)
+        nc.vector.tensor_tensor(own_down[:, POOL_END:], part[:, POOL_END:], own_ps[:, POOL_END:], ADD)
         nc.vector.tensor_tensor(half(up, 1), half(at_face, 1), sf_ps[:, P:], MULT)
-        own_head_up = part[:, HALF : HALF + P]
+        own_head_up = part[:, POOL_END : POOL_END + P]
         nc.vector.tensor_tensor(up[:, P:HALF], at_face[:, P:HALF], sf_ps[:, :P], MULT)
         nc.vector.tensor_tensor(own_head_up, part[:, :P], up[:, :P], ADD)
         for lo, hi in ((LAST_END, S), (P, LAST_END), (0, P)):

@@ -32,6 +32,7 @@ LAST_END = HALF + P // 2
 REGION = 32 * 1024
 SLOT = 4 * S
 POOL_END = P + 3 * P // 2
+DMA_ALIGN = 256
 Y_PIECES = ((0, HALF), (HALF, HALF + P), (HALF + P, S))
 
 
@@ -56,11 +57,11 @@ def tile_picked_yhodge_none_p_kernel(
             return tile
 
         def far_tile(name, shape, region, slot=0):
-            return apart.tile(shape, F32, name=name, offset=(region + 1) * REGION + slot * SLOT)
+            return apart.tile(shape, F32, name=name, offset=(region + 1) * REGION + slot * SLOT, align_bytes=DMA_ALIGN)
 
         def load_weight(name, src, tile=None):
             if tile is None:
-                tile = work.tile([P, PACK, N], F32, name=name)
+                tile = work.tile([P, PACK, N], F32, name=name, align_bytes=DMA_ALIGN)
             nc.sync.dma_start(tile[:], src.rearrange("(p j) n -> p j n", j=PACK))
             return tile
 
@@ -98,7 +99,7 @@ def tile_picked_yhodge_none_p_kernel(
         def half(tile, i):
             return tile[:, i * HALF : (i + 1) * HALF]
 
-        xs = work.tile([P, T], U8, name="xs", align_bytes=64)
+        xs = work.tile([P, T], U8, name="xs", align_bytes=DMA_ALIGN)
         nc.vector.memset(xs[:].bitcast(I32), 0)
         ident = work.tile([P, P], F32, name="ident")
         make_identity(nc, ident[:])
@@ -111,7 +112,7 @@ def tile_picked_yhodge_none_p_kernel(
                 xs[SCALE_START + r : P : QUADRANT_SIZE, :].bitcast(I32),
                 x_scales[0, r : QUADRANTS * SCALE_ROWS : SCALE_ROWS, :].bitcast(I32),
             )
-        xw = work.tile([P, T], U32, name="xw", align_bytes=64)
+        xw = work.tile([P, T], U32, name="xw", align_bytes=DMA_ALIGN)
         nc.sync.dma_start(xw[:].bitcast(I32), x_words[0].rearrange("p n t -> p (n t)").bitcast(I32))
         w2_raw = load_weight("w2_raw", w2, far_tile("w2_raw", [P, PACK, N], 0))
         w3_raw = load_weight("w3_raw", w3)
@@ -120,7 +121,7 @@ def tile_picked_yhodge_none_p_kernel(
         dv_win = far_tile("dv_win", [P, 3 * V], 2)
         sa_t, sb_t = dv_win[:, V : 2 * V], dv_win[:, 2 * V :]
         nc.sync.dma_start(sb_t, sb)
-        sn_first = work.tile([P, HALF], F32, name="sn_first")
+        sn_first = work.tile([P, HALF], F32, name="sn_first", align_bytes=DMA_ALIGN)
         nc.sync.dma_start(sn_first[:], half(sn, 0))
         cu_win = far_tile("cu_win", [P, 2 * V], 3)
         nc.sync.dma_start(cu_win[:, V:], half(sn, 1))
@@ -177,7 +178,7 @@ def tile_picked_yhodge_none_p_kernel(
         for i, signs in enumerate((sn_first[:], cu_win[:, V:])):
             nc.vector.tensor_tensor(half(li, i), y[:].indirect(half_list(inc_t, i)), signs, MULT)
         term_a = work.tile([P, V], F32, name="term_a")
-        term_b = work.tile([P, V], F32, name="term_b", tag="sn_first")
+        term_b = work.tile([P, V], F32, name="term_b", tag="sn_first", align_bytes=DMA_ALIGN)
 
         for i in range(2):
             pairs = half(li, i)
@@ -191,7 +192,7 @@ def tile_picked_yhodge_none_p_kernel(
         tail_b = far_tile("tail_b", [P, POOL_END - P], 4, 2)
         at_face = far_tile("at_face", [P, S], 4, 3)
         up = work.tile([P, S], F32, name="up")
-        result = work.tile([P, S], F32, name="result")
+        result = work.tile([P, S], F32, name="result", align_bytes=DMA_ALIGN)
         nc.scalar.activation(tail_second, dv_win[:].indirect(entries(tail_t, POOL_END, S)), COPY)
         nc.scalar.activation(tail_b[:], dv_win[:].indirect(entries(tail_t, P, POOL_END)), COPY)
         nc.vector.tensor_tensor(part[:, :P], dv_win[:].indirect(entries(head_t, 0, P)), own[:, :P], ADD)

@@ -56,8 +56,8 @@ def tile_picked_yhodge_none_p_kernel(
             nc.sync.dma_start(tile[:], src)
             return tile
 
-        def far_tile(name, shape, region, slot=0):
-            return apart.tile(shape, F32, name=name, offset=(region + 1) * REGION + slot * SLOT, align_bytes=DMA_ALIGN)
+        def far_tile(name, shape, region, slot=0, dtype=F32):
+            return apart.tile(shape, dtype, name=name, offset=(region + 1) * REGION + slot * SLOT, align_bytes=DMA_ALIGN)
 
         def load_weight(name, src, tile=None):
             if tile is None:
@@ -71,8 +71,8 @@ def tile_picked_yhodge_none_p_kernel(
             return grouped
 
         def quantise(name, grouped, tag):
-            codes = work.tile([P, N], U32, name=name + "_codes", tag=tag, align_bytes=64)
-            scales = work.tile([P, N], U8, name=name + "_scales", align_bytes=64)
+            codes = work.tile([P, N], U32, name=name + "_codes", tag=tag, align_bytes=DMA_ALIGN)
+            scales = work.tile([P, N], U8, name=name + "_scales", align_bytes=DMA_ALIGN)
             nc.vector.quantize_mx(
                 out=codes[:].bitcast(FP8X4), scales=scales[:], in_=grouped[:].rearrange("p n j -> p (n j)")
             )
@@ -128,7 +128,7 @@ def tile_picked_yhodge_none_p_kernel(
         inc_t = load_list("inc_t", inc)
         nc.sync.dma_start(sa_t, sa)
         head_t = load_list("head_t", head)
-        part = work.tile([P, S], F32, name="part")
+        part = far_tile("part", [P, S], 5, 2)
         sf_cols = part[:, P : P + SPREAD]
         with nc.allow_non_contiguous_dma(reason="one sign a partition and square"):
             nc.sync.dma_start(sf_cols, sf[0, P:].rearrange("(c p) -> p c", p=P))
@@ -138,14 +138,14 @@ def tile_picked_yhodge_none_p_kernel(
         face_t = load_list("face_t", face)
 
         w1_bf = round_weight("w1_bf", w1_raw, nc.vector.tensor_copy)
-        picked_scales = work.tile([P, S], U8, name="picked_scales", align_bytes=64)
+        picked_scales = work.tile([P, S], U8, name="picked_scales", align_bytes=DMA_ALIGN)
         nc.vector.tensor_copy(picked_scales[:], xs[:].indirect(offs_t[:]))
         w1_q = quantise("w1", w1_bf, "w1_codes")
 
-        w2_bf = work.tile([P, N, PACK], BF16, name="w2_bf", align_bytes=64)
+        w2_bf = work.tile([P, N, PACK], BF16, name="w2_bf", align_bytes=DMA_ALIGN)
         for copy, cols in ((nc.scalar.copy, slice(0, ROUND_SPLIT)), (nc.gpsimd.tensor_copy, slice(ROUND_SPLIT, N))):
             copy(w2_bf[:, cols, :], w2_raw[:, :, cols].rearrange("p j n -> p n j"))
-        picked_words = work.tile([P, S], U32, name="picked_words", align_bytes=64)
+        picked_words = far_tile("picked_words", [P, S], 5, 0, U32)
         y = far_tile("y", [P, S], 0)
         for lo, hi in Y_PIECES:
             nc.vector.tensor_copy(picked_words[:, lo:hi], xw[:].indirect(entries(offs_t, lo, hi)))
@@ -174,7 +174,7 @@ def tile_picked_yhodge_none_p_kernel(
         for c in range(SPREAD):
             nc.tensor.transpose(sf_ps[:, c * P : (c + 1) * P], sf_cols[:, c : c + 1].to_broadcast([P, P]), ident[:])
 
-        li = work.tile([P, S], F32, name="li")
+        li = far_tile("li", [P, S], 5, 1)
         for i, signs in enumerate((sn_first[:], cu_win[:, V:])):
             nc.vector.tensor_tensor(half(li, i), y[:].indirect(half_list(inc_t, i)), signs, MULT)
         term_a = work.tile([P, V], F32, name="term_a")
@@ -191,7 +191,7 @@ def tile_picked_yhodge_none_p_kernel(
         tail_second = own_down[:, P : P + S - POOL_END]
         tail_b = far_tile("tail_b", [P, POOL_END - P], 4, 2)
         at_face = far_tile("at_face", [P, S], 4, 3)
-        up = work.tile([P, S], F32, name="up")
+        up = far_tile("up", [P, S], 5, 3)
         result = work.tile([P, S], F32, name="result", align_bytes=DMA_ALIGN)
         nc.scalar.activation(tail_second, dv_win[:].indirect(entries(tail_t, POOL_END, S)), COPY)
         nc.scalar.activation(tail_b[:], dv_win[:].indirect(entries(tail_t, P, POOL_END)), COPY)

from contextlib import ExitStack

import concourse.mybir as mybir
from concourse.masks import make_identity

K, T, S, N, V = 512, 2048, 512, 128, 256
FLOPS = 3 * 2 * K * N * S

F32 = mybir.dt.float32
BF16 = mybir.dt.bfloat16
I32 = mybir.dt.int32
U32 = mybir.dt.uint32
U16 = mybir.dt.uint16
U8 = mybir.dt.uint8
FP8X4 = mybir.dt.float8_e4m3fn_x4
MULT = mybir.AluOpType.mult
ADD = mybir.AluOpType.add
SUB = mybir.AluOpType.subtract
COPY = mybir.ActivationFunctionType.Copy

P = 128
PACK = 4
QUADRANTS = 4
QUADRANT_SIZE = P // QUADRANTS
SCALE_ROWS = 4
SCALE_START = 12
LIST_COL = 16
HALF = S // 2
SPREAD = S // P - 1
ROUND_SPLIT = 3 * N // 4
LAST_END = HALF + P // 2
REGION = 32 * 1024
SLOT = 4 * S
POOL_END = P + 3 * P // 2
DMA_ALIGN = 256
Y_PIECES = ((0, HALF), (HALF, HALF + P), (HALF + P, S))


def tile_picked_yhodge_none_p_kernel(
    tc, x_words, x_scales, w1, w2, w3, sn, sa, sb, sf, offs, inc, head, tail, tri, trj, face, out
):
    nc = tc.nc
    with ExitStack() as ctx:
        lists = ctx.enter_context(tc.tile_pool(name="lists", bufs=1))
        work = ctx.enter_context(tc.tile_pool(name="work", bufs=1))
        apart = ctx.enter_context(tc.tile_pool(name="apart", bufs=1))
        psum = ctx.enter_context(tc.psum_pool(name="psum", bufs=1))

        def load_list(name, src):
            tile = lists.tile(list(src.shape), U16, name=name)
            nc.sync.dma_start(tile[:], src)
            return tile

        def load_signs(name, src):
            tile = work.tile(list(src.shape), F32, name=name)
            nc.sync.dma_start(tile[:], src)
            return tile

        def far_tile(name, shape, region, slot=0, dtype=F32):
            return apart.tile(shape, dtype, name=name, offset=(region + 1) * REGION + slot * SLOT, align_bytes=DMA_ALIGN)

        def load_weight(name, src, tile=None):
            if tile is None:
                tile = work.tile([P, PACK, N], F32, name=name, align_bytes=DMA_ALIGN)
            nc.sync.dma_start(tile[:], src.rearrange("(p j) n -> p j n", j=PACK))
            return tile

        def round_weight(name, raw, copy):
            grouped = work.tile([P, N, PACK], BF16, name=name, align_bytes=64)
            copy(grouped[:], raw[:].rearrange("p j n -> p n j"))
            return grouped

        def quantise(name, grouped, tag):
            codes = work.tile([P, N], U32, name=name + "_codes", tag=tag, align_bytes=DMA_ALIGN)
            scales = work.tile([P, N], U8, name=name + "_scales", align_bytes=DMA_ALIGN)
            nc.vector.quantize_mx(
                out=codes[:].bitcast(FP8X4), scales=scales[:], in_=grouped[:].rearrange("p n j -> p (n j)")
            )
            return codes, scales

        def product(dst, weight, words, scales):
            w_codes, w_scales = weight
            nc.tensor.matmul_mx(
                out=dst,
                lhsT=w_codes[:].bitcast(FP8X4),
                lhsT_scale=w_scales[:],
                rhs=words.bitcast(FP8X4),
                rhs_scale=scales,
                start=True,
                stop=True,
            )

        def entries(tile, lo, hi):
            return tile[:, lo // LIST_COL : hi // LIST_COL]

        def half_list(tile, i):
            return entries(tile, i * HALF, (i + 1) * HALF)

        def half(tile, i):
            return tile[:, i * HALF : (i + 1) * HALF]

        xs = work.tile([P, T], U8, name="xs", align_bytes=DMA_ALIGN)
        nc.vector.memset(xs[:].bitcast(I32), 0)
        ident = work.tile([P, P], F32, name="ident")
        make_identity(nc, ident[:])

        w1_raw = load_weight("w1_raw", w1)
        offs_t = load_list("offs_t", offs)
        for r in range(SCALE_ROWS):
            queue = nc.sync if r < SCALE_ROWS // 2 else nc.scalar
            queue.dma_start(
                xs[SCALE_START + r : P : QUADRANT_SIZE, :].bitcast(I32),
                x_scales[0, r : QUADRANTS * SCALE_ROWS : SCALE_ROWS, :].bitcast(I32),
            )
        xw = work.tile([P, T], U32, name="xw", align_bytes=DMA_ALIGN)
        nc.sync.dma_start(xw[:].bitcast(I32), x_words[0].rearrange("p n t -> p (n t)").bitcast(I32))
        w2_raw = load_weight("w2_raw", w2, far_tile("w2_raw", [P, PACK, N], 0))
        w3_raw = load_weight("w3_raw", w3)
        tri_t = load_list("tri_t", tri)
        trj_t = load_list("trj_t", trj)
        dv_win = far_tile("dv_win", [P, 3 * V], 2)
        sa_t, sb_t = dv_win[:, V : 2 * V], dv_win[:, 2 * V :]
        nc.sync.dma_start(sb_t, sb)
        sn_first = work.tile([P, HALF], F32, name="sn_first", align_bytes=DMA_ALIGN)
        nc.sync.dma_start(sn_first[:], half(sn, 0))
        cu_win = far_tile("cu_win", [P, 2 * V], 3)
        nc.sync.dma_start(cu_win[:, V:], half(sn, 1))
        inc_t = load_list("inc_t", inc)
        nc.sync.dma_start(sa_t, sa)
        head_t = load_list("head_t", head)
        part = far_tile("part", [P, S], 5, 2)
        sf_cols = part[:, P : P + SPREAD]
        with nc.allow_non_contiguous_dma(reason="one sign a partition and square"):
            nc.sync.dma_start(sf_cols, sf[0, P:].rearrange("(c p) -> p c", p=P))
        sf_t = far_tile("sf_t", [P, P], 4, 4)
        nc.sync.dma_start(sf_t[:], sf[:, :P])
        tail_t = load_list("tail_t", tail)
        face_t = load_list("face_t", face)

        w1_bf = round_weight("w1_bf", w1_raw, nc.vector.tensor_copy)
        picked_scales = work.tile([P, S], U8, name="picked_scales", align_bytes=DMA_ALIGN)
        nc.vector.tensor_copy(picked_scales[:], xs[:].indirect(offs_t[:]))
        w1_q = quantise("w1", w1_bf, "w1_codes")

        w2_bf = work.tile([P, N, PACK], BF16, name="w2_bf", align_bytes=DMA_ALIGN)
        for copy, cols in ((nc.scalar.copy, slice(0, ROUND_SPLIT)), (nc.gpsimd.tensor_copy, slice(ROUND_SPLIT, N))):
            copy(w2_bf[:, cols, :], w2_raw[:, :, cols].rearrange("p j n -> p n j"))
        picked_words = far_tile("picked_words", [P, S], 5, 0, U32)
        y = far_tile("y", [P, S], 0)
        for lo, hi in Y_PIECES:
            nc.vector.tensor_copy(picked_words[:, lo:hi], xw[:].indirect(entries(offs_t, lo, hi)))
        for piece, (lo, hi) in enumerate(Y_PIECES):
            y_ps = psum.tile([P, hi - lo], F32, name="y_ps%d" % piece)
            product(y_ps[:], w1_q, picked_words[:, lo:hi], picked_scales[SCALE_START:, lo:hi])
            nc.scalar.copy(y[:, lo:hi], y_ps[:])

        w3_bf = round_weight("w3_bf", w3_raw, nc.vector.tensor_copy)
        w2_q = quantise("w2", w2_bf, "w2_codes")
        h = far_tile("h", [P, S], 1)
        for piece, (lo, hi) in enumerate(Y_PIECES):
            h_ps = psum.tile([P, hi - lo], F32, name="h_ps%d" % piece)
            product(h_ps[:], w2_q, picked_words[:, lo:hi], picked_scales[SCALE_START:, lo:hi])
            nc.scalar.copy(h[:, lo:hi], h_ps[:])

        w3_q = quantise("w3", w3_bf, "w2_bf")
        curl_a = far_tile("curl_a", [P, V], 4)
        nc.scalar.activation(curl_a[:], h[:].indirect(tri_t[:]), COPY)
        own = far_tile("own", [P, POOL_END], 0)
        own_ps = psum.tile([P, S], F32, name="own_ps")
        product(own_ps[:], w3_q, picked_words[:], picked_scales[SCALE_START:, :])
        nc.scalar.copy(own[:], own_ps[:, :POOL_END])

        sf_ps = psum.tile([P, SPREAD * P], F32, name="sf_ps")
        for c in range(SPREAD):
            nc.tensor.transpose(sf_ps[:, c * P : (c + 1) * P], sf_cols[:, c : c + 1].to_broadcast([P, P]), ident[:])

        li = far_tile("li", [P, S], 5, 1)
        for i, signs in enumerate((sn_first[:], cu_win[:, V:])):
            nc.vector.tensor_tensor(half(li, i), y[:].indirect(half_list(inc_t, i)), signs, MULT)
        term_a = work.tile([P, V], F32, name="term_a")
        term_b = work.tile([P, V], F32, name="term_b", tag="sn_first", align_bytes=DMA_ALIGN)

        for i in range(2):
            pairs = half(li, i)
            cols = slice(i * P, (i + 1) * P)
            nc.vector.tensor_tensor(dv_win[:, cols], pairs[:, 0::2], pairs[:, 1::2], ADD)
            nc.vector.tensor_tensor(term_b[:, cols], h[:].indirect(entries(trj_t, cols.start, cols.stop)), sb_t[:, cols], MULT)
        nc.vector.tensor_tensor(term_a[:], curl_a[:], sa_t, MULT)

        own_down = far_tile("own_down", [P, S], 4, 1)
        tail_second = own_down[:, P : P + S - POOL_END]
        tail_b = far_tile("tail_b", [P, POOL_END - P], 4, 2)
        at_face = far_tile("at_face", [P, S], 4, 3)
        up = far_tile("up", [P, S], 5, 3)
        result = work.tile([P, S], F32, name="result", align_bytes=DMA_ALIGN)
        nc.scalar.activation(tail_second, dv_win[:].indirect(entries(tail_t, POOL_END, S)), COPY)
        nc.scalar.activation(tail_b[:], dv_win[:].indirect(entries(tail_t, P, POOL_END)), COPY)
        nc.vector.tensor_tensor(part[:, :P], dv_win[:].indirect(entries(head_t, 0, P)), own[:, :P], ADD)
        nc.vector.tensor_tensor(cu_win[:, :V], term_a[:], term_b[:], ADD)
        nc.vector.tensor_tensor(part[:, P:POOL_END], dv_win[:].indirect(entries(head_t, P, POOL_END)), own[:, P:], ADD)
        nc.vector.tensor_tensor(part[:, POOL_END:], dv_win[:].indirect(entries(head_t, POOL_END, S)), tail_second, SUB)
        for lo, hi in ((HALF, S), (P, HALF)):
            nc.scalar.activation(at_face[:, lo:hi], cu_win[:].indirect(entries(face_t, lo, hi)), COPY)
        nc.vector.tensor_tensor(up[:, :P], cu_win[:].indirect(entries(face_t, 0, P)), sf_t[:], MULT)
        nc.scalar.activation(sf_t[:], dv_win[:].indirect(entries(tail_t, 0, P)), COPY)
        nc.gpsimd.tensor_tensor(own_down[:, P:POOL_END], part[:, P:POOL_END], tail_b[:], SUB)
        nc.vector.tensor_tensor(own_down[:, POOL_END:], part[:, POOL_END:], own_ps[:, POOL_END:], ADD)
        nc.vector.tensor_tensor(half(up, 1), half(at_face, 1), sf_ps[:, P:], MULT)
        own_head_up = part[:, POOL_END : POOL_END + P]
        nc.vector.tensor_tensor(up[:, P:HALF], at_face[:, P:HALF], sf_ps[:, :P], MULT)
        nc.vector.tensor_tensor(own_head_up, part[:, :P], up[:, :P], ADD)
        for lo, hi in ((LAST_END, S), (P, LAST_END), (0, P)):
            if lo == 0:
                nc.vector.tensor_tensor(result[:, :P], own_head_up, sf_t[:], SUB)
            else:
                nc.vector.tensor_tensor(result[:, lo:hi], own_down[:, lo:hi], up[:, lo:hi], ADD)
            nc.sync.dma_start(out[:, lo:hi], result[:, lo:hi])
